import numpy as np, ml_dtypes
CORES = [3,11,19,27,35,43,51,59]
N = 8
import mx_ref
BF = ml_dtypes.bfloat16
def cols(t, e):
    v = np.concatenate([t.reshape(128, -1, 4), np.zeros((128, 1, 4), BF)], axis=1)
    return np.ascontiguousarray(v[:, e]).reshape(128, -1)
def f(rng, *shape):
    return mx_ref.flush((rng.standard_normal(shape, dtype=np.float32) * np.exp2(rng.integers(-2, 3, shape[:-1] + (1,)))).astype(BF))
def wide(rng, *shape, cols=0):
    v = rng.standard_normal(shape, dtype=np.float32) * np.exp2(rng.integers(-12, 13, shape)).astype(np.float32)
    if cols: v *= np.repeat(np.exp2(rng.integers(-cols, cols + 1, shape[:-2] + (1, shape[-1] // 4))) * (rng.random(shape[:-2] + (1, shape[-1] // 4)) > 0.0625), 4, axis=-1).astype(np.float32)
    return mx_ref.flush(v.astype(BF))
T, K, O = 512, 128, 3
def setup_inputs(rng):
    u = np.zeros((128, 512), BF); u[:, :4] = f(rng, 128, 4)
    return {"x": f(rng, N, 128, 4 * T), "u": np.stack([u] * N), "w": f(rng, N, 128, 512 * O)}
def signs(d):
    return np.where(d["u"][0][:, :4].astype(np.float32) < 0, -1, 1).astype(np.float32)
def blocks(rng, n):
    return np.repeat(rng.permutation(16) < n, 8)
def plant(rng, d, n):
    for s in range(N):
        v = d["x"][s].astype(np.float32).reshape(128, T, 4)
        k = rng.permutation(T)[:n[s]]
        v[:, k] = np.abs(v[:, k]) * signs(d)[:, None] * np.float32(8)
        d["x"][s] = v.reshape(128, -1).astype(BF)
    return d
def setup_inputs_one(rng):
    d = setup_inputs(rng); return plant(rng, d, np.where(np.arange(N) == rng.integers(0, N), K, 0))
def setup_inputs_zeros(rng):
    d = setup_inputs(rng); m = blocks(rng, 2)
    d["u"][:, ~m] = 0
    k = rng.permutation(N * T); g = np.full(N * T, -1, np.float32)
    g[k[:K // 3]] = 1; g[k[K // 3:2 * (K // 3)]] = 0
    v = np.abs(d["x"][:, m].astype(np.float32)).reshape(N, -1, T, 4)
    d["x"][:, m] = (v * signs(d)[m][:, None] * g.reshape(N, 1, T, 1)).reshape(N, -1, 4 * T).astype(BF)
    return d
def setup_inputs_few(rng):
    d = setup_inputs(rng); p = rng.permutation(N); g = p[N - N // 2:]
    d["x"][g] = (-np.abs(d["x"][g].astype(np.float32)) * np.tile(signs(d), (1, T))).astype(BF)
    n = np.zeros(N, int); n[p[:2]] = [K * 3 // 5, K - K * 3 // 5]
    return plant(rng, d, n)
def setup_inputs_ties(rng):
    d = setup_inputs(rng); b = f(rng, 128, 4 * 80); m = blocks(rng, 4)
    d["u"][:, m] = 0
    d["x"] = np.stack([cols(b, rng.permutation(np.arange(T) % 80)) for r in range(N)])
    d["x"][:, m] = f(rng, N, 32, 4 * T); return d
def setup_inputs_spread(rng):
    d = setup_inputs(rng); d["x"] = wide(rng, N, 128, 4 * T, cols=8); return d
def check_inputs(d):
    b = []
    u = d["u"].astype(np.float32)
    if (u != u[:1]).any(): b.append("u_same")
    if (u[:, :, 4:] != 0).any(): b.append("u_zero")
    return b
def reference(x, u, w):
    s = np.stack([mx_ref.matmul(mx_ref.quantize(u[r]), mx_ref.quantize(x[r]))[0] for r in range(N)]).reshape(-1) + np.float32(0.0)
    best = np.lexsort((np.arange(N * T), -s))[:K]
    V = mx_ref.quantize(cols(np.concatenate(list(x), axis=1), best))
    y = np.zeros((N, 128, O * K), np.float32)
    for r in range(N):
        for o in range(O): y[r][:, K * o:K * o + K] = mx_ref.matmul(mx_ref.quantize(np.ascontiguousarray(w[r][:, 512 * o:512 * o + 512])), V)
    who = np.stack([best // T, best % T]).astype(np.float32)
    return {"y": y, "id": np.stack([who] * N)}

@@ -1,0 +1,269 @@
+from concourse.bass import DstId, RemoteDMATransfer
+from concourse.mybir import dt, AluOpType as A, ActivationFunctionType as F, AxisListType
+
+N, NB, K2, BIG = 8, 16, 32, 1.0e29
+SCRATCH = {"psb": ("psum", [128, 2048], "float32"), "pss": ("psum", [128, 2048], "float32")}
+for _d, _l in (("float8_e4m3fn_x4", "xq 512 uq 128 ur 128 wq 384 snd1 128 land1 128 snd2 32 land2 256"),
+               ("uint8", "xs 512 us 128 urs 128 ws 384 snd1s 128 land1s 128 snd2s 32 land2s 256"),
+               ("bfloat16", "xb 2048 ub 512 wb 1536 k2 96 k3 256 jb 4 g1 2560 r1 1280 g2 256 g3 1024 r3 512 oh3 512 ot3 512"),
+               ("uint16", "zoff 8 off1 8 off2 2 off3 8"), ("int32", "l2 3 i2x 2 vg 128 wi 128 ji 128"),
+               ("float32", "z32 32 zt 128 tri 128 on8 8 m8a 8 m8 8 sc1 4 st1 512 qa1 8 qb1 8 l1 8 lid 8 hid1 8 idl 32 sc2 1 st2 128 r2 128 m9 9 vp 1"
+                " oh2 96 ot2 96 p2 3 qa2 3 qb2 3 vs 1 hid2 1 vl 32 xr 256 idr 256 idc 2 tie 512 sc3 2 st3 512 qa3 8 qb3 8 l3 8 ysb 768 yo 384 wf 128 jf 128")):
+    _w = _l.split()
+    for _i in range(0, len(_w), 2):
+        SCRATCH[_w[_i]] = ("sbuf", [128, int(_w[_i + 1])], _d)
+for _n, _k in (("krow", 32), ("oh1", 128), ("ot1", 128), ("sm1", 64), ("sm3", 32)):
+    SCRATCH[_n] = ("sbuf", [128, 8, _k], "bfloat16")
+SEMAPHORES = "vec sca ten pool du dx0 dx1 dx2 dx3 dw a1 a2 n1 n2 h1 h2 loc dy0 dy1 dy2 di0 di1".split()
+
+
+def helper_of(core, T, topo):
+    c = [h for h in topo.cores_of(core) if T.rank_of(h) is None and all(topo.may_write(h, d) for d in T.cores)]
+    return sorted(c, key=lambda h: (topo.die(h) != topo.die(core), h))[0]
+
+
+def near_engines(core, h, T, topo):
+    far = [d for d in T.cores if d != core]
+    return [e for e in topo.engines(core, h) if e not in topo.engines(core, far[0])][0:4]
+
+
+def slot2(r):
+    return 4 * (r % 2) + r // 2
+
+
+def to_all(g, core, r, first, sem, src, dst, T, topo):
+    tr = []
+    for b in range(1, N):
+        d = T.cores[(r + b) % N]
+        rid, pid = topo.addr(d)[0:2]
+        tr.append(RemoteDMATransfer(dst_ids=[DstId(rid=rid, pnc=pid)], dma_engine_mask=1 << topo.engines(core, d)[b - 1 + first], remote_sem=T.sem[sem], src=src(b), dst=dst))
+    g.remote_dma_fused(tr, local_sem=T.sem.loc)
+
+
+def hand_on(g, core, r, T, topo):
+    n = len(near_engines(T.cores[r], core, T, topo))
+    g.wait_ge(T.sem.h1, n)
+    to_all(g, core, r, 0, "n1", lambda b: T.hid1[:, b:b + 1], T.idl[:, 4 * r:4 * r + 1], T, topo)
+    g.wait_ge(T.sem.h2, n)
+    to_all(g, core, r, 0, "n2", lambda b: T.hid2[:], T.vl[:, 4 * slot2(r):4 * slot2(r) + 1], T, topo)
+    g.wait_ge(T.sem.loc, 2 * (N - 1))
+
+
+def rank_program(g, core, T, topo):
+    S, rank = T.sem, T.rank_of(core)
+    if rank is None:
+        for r in range(N):
+            if helper_of(T.cores[r], T, topo) == core:
+                hand_on(g, core, r, T, topo)
+        return
+    q = {"vec": g.vector, "sca": g.scalar, "ten": g.tensor, "pool": g, "sync": g.sync}
+    v = g.vector
+    ops = {"copy": v.tensor_copy, "tt": v.tensor_tensor, "ts": v.tensor_scalar, "red": v.tensor_reduce, "scan": v.tensor_tensor_scan,
+           "tr": v.transpose, "set": v.memset, "qz": v.quantize_mx}
+    cnt, seen = {}, {}
+
+    def need(e, toks):
+        best = {}
+        for s, n in toks:
+            best[s] = max(best.get(s, 0), n)
+        for s in best:
+            if seen.get((e, s), 0) < best[s]:
+                q[e].wait_ge(S[s], best[s])
+                seen[(e, s)] = best[s]
+
+    def done(e, ins):
+        cnt[e] = cnt.get(e, 0) + 1
+        ins.then_inc(S[e], 1)
+        return (e, cnt[e])
+
+    def V(toks, name, *a):
+        need("vec", toks)
+        return done("vec", ops[name](*a))
+
+    def ACT(toks, *a, **k):
+        need("sca", toks)
+        return done("sca", g.scalar.activation(*a, **k))
+
+    def MM(toks, out, l, r):
+        need("ten", toks)
+        return done("ten", g.tensor.matmul_mx(out, l[0], l[1], r[0], r[1], True, True))
+
+    def P(*a):
+        return done("pool", g.affine_select(*a))
+
+    def IOTA(*a):
+        return done("pool", g.iota(*a, allow_small_or_imprecise_dtypes=True))
+
+    def dma(e, toks, out, in_, sem):
+        need(e, toks)
+        q[e].dma_start(out, in_).then_inc(S[sem], 16)
+        return (sem, 16)
+
+    def u32(ap):
+        return ap.bitcast(dt.uint32)
+
+    def c128(i, w=128):
+        return slice(w * i, w * i + w)
+
+    du = dma("sca", [], T.ub[:], T.u[:], "du")
+    dx = [dma(("sync", "sca")[i % 2], [], T.xb[:, c128(i, 512)], T.x[:, c128(i, 512)], "dx%d" % i) for i in range(4)]
+    dw = dma("sync", [], T.wb[:], T.w[:], "dw")
+
+    c_zoff = V([], "set", T.zoff[:], 0)
+    c_zt = V([], "set", T.zt[:], 0.0)
+    c_on = V([], "set", T.on8[:], 1.0)
+    c_z32 = V([], "set", T.z32[:], 0.0)
+    need("pool", [c_zt, c_on])
+    c_tri = P(T.tri[:], T.zt[:], [[-1, 128]], A.is_gt, BIG, 0, 1)
+    IOTA(T.jb[:], [[128, 4]], -256, 1)
+    c_kr = IOTA(T.krow[:], [[1, 8], [0, 2], [8, 16]], 0, 0)
+    c_ma = P(T.m8a[:], T.on8[:], [[-16, 8]], A.is_ge, 0.0, 0, 1)
+    need("pool", [c_ma])
+    P(T.m8[:], T.m8a[:], [[16, 8]], A.is_ge, 0.0, 15, -1)
+    IOTA(T.m9[:, 8:9], [[0, 1]], 0, 1)
+    IOTA(T.k2[:, 0:64], [[16, 2], [0, 2], [1, 16]], 0, 0)
+    IOTA(T.k2[:, 64:96], [[1, 32]], 0, 0)
+    c_k3 = IOTA(T.k3[:], [[16, 8], [0, 2], [1, 16]], 0, 0)
+
+    t = V([du], "qz", T.uq[:], T.us[:], T.ub[:])
+    c_ur = V([t, c_zoff], "copy", u32(T.ur[:]), u32(T.uq[:]).indirect(T.zoff[:]))
+    c_us = ACT([t, c_zoff], T.urs[:], T.us[:].indirect(T.zoff[:]), F.Copy)
+    U = (T.ur[:], T.urs[:])
+
+    tq, tB, sc, st, rk, oh, last = {}, {}, {}, {}, {}, {}, {}
+
+    def quant(i):
+        X = (T.xq[:, c128(i)], T.xs[:, c128(i)])
+        tq[i] = V([dx[i]], "qz", X[0], X[1], T.xb[:, c128(i, 512)])
+        t = MM([tq[i], c_ur, c_us], T.pss[:, 512 * i:512 * i + 128], X, U)
+        tB[i] = MM([], T.psb[:, 512 * i:512 * i + 128], U, X)
+        sc[i] = ACT([t], T.sc1[:, i:i + 1], T.pss[:, 512 * i:512 * i + 1], F.Copy)
+        st[i] = ACT([sc[i], c_tri], T.st1[:, c128(i)], T.tri[:], F.Identity, bias=T.sc1[:, i:i + 1])
+
+    def blocks(*ci):
+        for c, i in ci:
+            last[c] = V([tB[i], sc[c]], "ts", T.g1[:, 640 * c + 128 * i:640 * c + 128 * i + 128], T.psb[:, 512 * i:512 * i + 128], T.sc1[:, c:c + 1], None, A.is_ge if i < c else A.is_gt)
+
+    def equal(c):
+        last[c] = V([tB[c], st[c]], "tt", T.g1[:, 640 * c + 512:640 * c + 640], T.psb[:, 512 * c:512 * c + 128], T.st1[:, c128(c)], A.is_equal)
+
+    def count(c):
+        rk[c] = V([last[c]], "scan", T.r1[:, c128(c, 320)], T.g1[:, 640 * c:640 * c + 320], T.g1[:, 640 * c + 320:640 * c + 640], 0.0, A.add, A.add)
+
+    quant(0)
+    quant(1)
+    blocks((0, 0), (0, 1), (1, 0), (1, 1))
+    quant(2)
+    equal(0)
+    equal(1)
+    blocks((0, 2), (1, 2), (2, 0), (2, 1), (2, 2))
+    quant(3)
+    equal(2)
+    blocks((0, 3), (1, 3), (2, 3), (3, 0), (3, 1), (3, 2), (3, 3))
+    for c in range(3):
+        count(c)
+    equal(3)
+    count(3)
+    free1 = [last[3]] + list(sc.values())
+    for c in range(4):
+        oh[c] = V([rk[c], c_kr], "ts", T.oh1[:, :, c128(c, 32)], T.krow[:], T.r1[:, 320 * c + 319:320 * c + 320], T.jb[:, c:c + 1], A.is_equal, A.mult)
+    tr = [V(list(oh.values()), "tr", T.ot1[:, b, :], T.oh1[:, b, :]) for b in range(8)]
+    sm = [V([tr[b]], "scan", T.sm1[:, b, :], T.ot1[:, b, 0:64], T.ot1[:, b, 64:128], 0.0, A.add, A.add) for b in range(8)]
+
+    def fold(toks, src, qa, qb, dst):
+        t0 = V(toks, "tt", qa[0:32, :], src(0), src(32), A.add)
+        t1 = V(toks, "tt", qb[0:32, :], src(64), src(96), A.add)
+        return [V([t0, t1], "tt", dst[a:a + 32, :], qa[0:32, :], qb[0:32, :], A.add) for a in (0, 32, 64, 96)]
+
+    l1 = fold(sm, lambda a: T.sm1[a:a + 32, :, 63], T.qa1, T.qb1, T.l1)
+    off1 = V(l1, "ts", T.off1[:], T.l1[:], 256.0, None, A.add)
+    lid = ACT(l1, T.lid[:], T.l1[:], F.Identity, bias=65536.0 * rank + 32768.0, scale=128.0)
+    me1 = c128(rank, NB)
+    pc = V([off1], "copy", u32(T.snd1[:]), u32(T.xq[:]).indirect(T.off1[:]))
+    psc = ACT([off1], T.snd1s[:], T.xs[:].indirect(T.off1[:]), F.Copy)
+    oc = V([], "copy", u32(T.land1[:, me1]), u32(T.xq[:]).indirect(T.off1[:, 0:1]))
+    osc = ACT([], T.land1s[:, me1], T.xs[:].indirect(T.off1[:, 0:1]), F.Copy)
+    oid = ACT(l1, T.idl[:, 4 * rank:4 * rank + 1], T.l1[:, 0:1], F.Identity, bias=65536.0 * rank + 32768.0, scale=128.0)
+
+    h = helper_of(core, T, topo)
+    hrid, hpid = topo.addr(h)[0:2]
+    near = near_engines(core, h, T, topo)
+
+    def send(tok, out, in_, sem):
+        need("pool", [tok])
+        g.remote_dma(out, in_, S[sem], S.loc, hpid, hrid, sum(1 << e for e in near))
+
+    send(lid, T.hid1[:], T.lid[:], "h1")
+    need("pool", [pc])
+    to_all(g, core, rank, 0, "a1", lambda b: T.snd1[:, c128(b, NB)].bitcast(dt.uint8), T.land1[:, me1].bitcast(dt.uint8), T, topo)
+    need("pool", [psc])
+    to_all(g, core, rank, 1, "a1", lambda b: T.snd1s[:, c128(b, NB)], T.land1s[:, me1], T, topo)
+
+    wq = V([dw], "qz", T.wq[:], T.ws[:], T.wb[:])
+
+    arr1 = [("a1", 14), oc, osc]
+    L1 = (T.land1[:], T.land1s[:])
+    t = MM(arr1 + free1, T.pss[:, 0:128], L1, U)
+    tB2 = MM([], T.psb[:, 0:128], U, L1)
+    sc2 = ACT([t], T.sc2[:], T.pss[:, 0:1], F.Copy)
+    st2 = ACT([sc2], T.st2[:], T.tri[:], F.Identity, bias=T.sc2[:])
+    V([tB2, sc2], "ts", T.g2[:, 0:128], T.psb[:, 0:128], T.sc2[:], None, A.is_gt)
+    e2 = V([st2], "tt", T.g2[:, 128:256], T.psb[:, 0:128], T.st2[:], A.is_equal)
+    t = V([("n1", 7), oid, c_k3], "tt", T.m9[:, 0:8], T.idl[:, 0:32:4], T.m8[:], A.mult)
+    r2 = V([e2], "scan", T.r2[:], T.g2[:, 0:128], T.g2[:, 128:256], 0.0, A.add, A.add)
+    vp = V([t], "red", T.vp[:], T.m9[:], AxisListType.X, A.add)
+    t = V([r2, vp], "ts", T.oh2[:], T.k2[:], T.r2[:, 127:128], T.vp[:], A.is_equal, A.mult)
+    t = V([t], "tr", T.ot2[:], T.oh2[:])
+    p2 = [V([t], "red", T.p2[:, b:b + 1], T.ot2[:, c128(b, 32)], AxisListType.X, A.add) for b in range(3)]
+    l2 = fold(p2, lambda a: T.p2[a:a + 32, :], T.qa2, T.qb2, T.l2)
+    t = V(l2, "ts", T.i2x[:], T.l2[:, 0:2], 127, None, A.bitwise_and)
+    vs = V(l2, "copy", T.vs[:], T.l2[:, 2:3])
+    off2 = V([t], "copy", T.off2[:], T.i2x[:])
+    b2 = slot2(rank)
+    me2 = c128(b2, K2)
+    pc = V([off2] + arr1, "copy", u32(T.snd2[:]), u32(T.land1[:]).indirect(T.off2[:]))
+    psc = ACT([off2] + arr1, T.snd2s[:], T.land1s[:].indirect(T.off2[:]), F.Copy)
+    oc2 = V([], "copy", u32(T.land2[:, me2]), u32(T.land1[:]).indirect(T.off2[:]))
+    osc2 = ACT([], T.land2s[:, me2], T.land1s[:].indirect(T.off2[:]), F.Copy)
+    ov = V(l2, "copy", T.vl[:, 4 * b2:4 * b2 + 1], T.l2[:, 2:3])
+    send(vs, T.hid2[:], T.vs[:], "h2")
+    need("pool", [pc])
+    to_all(g, core, rank, 0, "a2", lambda b: T.snd2[:].bitcast(dt.uint8), T.land2[:, me2].bitcast(dt.uint8), T, topo)
+    need("pool", [psc])
+    to_all(g, core, rank, 1, "a2", lambda b: T.snd2s[:], T.land2s[:, me2], T, topo)
+
+    xr = [ACT([("n2", 7), ov, c_z32], T.xr[:, c128(b, 32)], T.z32[:], F.Identity, bias=T.vl[:, 4 * b:4 * b + 1]) for b in range(8)]
+    idc = [V([("n2", 7), ov], "copy", T.idc[32 * a:32 * a + 32, :], T.vl[32 * a:32 * a + 32, 4 * a:32:16]) for a in range(4)]
+    idr = V(xr, "tr", T.idr[:], T.xr[:])
+    tie = [V([idr] + idc, "ts", T.tie[:, c128(c, 256)], T.idr[:], T.idc[:, c:c + 1], BIG, A.is_ge, A.mult) for c in range(2)]
+
+    arr2 = [("a2", 14), oc2, osc2]
+    L2 = (T.land2[:], T.land2s[:])
+    tS3 = [MM(arr2 + [e2, sc2] + free1, T.pss[:, 512 * c + 512:512 * c + 640], (T.land2[:, c128(c)], T.land2s[:, c128(c)]), U) for c in range(2)]
+    b3 = T.psb[:, 512:768]
+    tB3 = MM([], b3, U, L2)
+    yps = [T.psb[:, 1024:1280], T.psb[:, 1536:1792], T.pss[:, 1536:1792]]
+    tY = [MM([wq], yps[o], (T.wq[:, c128(o)], T.ws[:, c128(o)]), L2) for o in range(3)]
+    sc3 = [ACT([tS3[c]], T.sc3[:, c:c + 1], T.pss[:, 512 * c + 512:512 * c + 513], F.Copy) for c in range(2)]
+    st3 = [ACT([sc3[c], tie[c]], T.st3[:, c128(c, 256)], T.tie[:, c128(c, 256)], F.Identity, bias=T.sc3[:, c:c + 1]) for c in range(2)]
+    ysb = [ACT([tY[o]], T.ysb[:, c128(o, 256)], yps[o], F.Copy) for o in range(3)]
+    g3 = [V([tB3, sc3[c]], "ts", T.g3[:, 512 * c:512 * c + 256], b3, T.sc3[:, c:c + 1], None, A.is_gt) for c in range(2)]
+    e3 = [V([st3[c]], "tt", T.g3[:, 512 * c + 256:512 * c + 512], b3, T.st3[:, c128(c, 256)], A.is_equal) for c in range(2)]
+    r3 = [V([g3[c], e3[c]], "scan", T.r3[:, c128(c, 256)], T.g3[:, 512 * c:512 * c + 256], T.g3[:, 512 * c + 256:512 * c + 512], 0.0, A.add, A.add) for c in range(2)]
+    oh3 = [V([r3[c]], "ts", T.oh3[:, c128(c, 256)], T.k3[:], T.r3[:, 256 * c + 255:256 * c + 256], T.jb[:, c + 2:c + 3], A.is_equal, A.mult) for c in range(2)]
+    t = V(oh3, "tr", T.ot3[:], T.oh3[:])
+    sm3 = [V([t], "scan", T.sm3[:, b, :], T.ot3[:, c128(b, 32)], T.ot3[:, 256 + 32 * b:288 + 32 * b], 0.0, A.add, A.add) for b in range(8)]
+    l3 = fold(sm3, lambda a: T.sm3[a:a + 32, :, 31], T.qa3, T.qb3, T.l3)
+    off3 = V(l3, "copy", T.off3[:], T.l3[:])
+    y0 = V([off3] + ysb, "copy", T.yo[:, c128(0)], T.ysb[:, 0:256].indirect(T.off3[:]))
+    y1 = ACT([off3] + ysb, T.yo[:, c128(1)], T.ysb[:, 256:512].indirect(T.off3[:]), F.Copy)
+    y2 = ACT([], T.yo[:, c128(2)], T.ysb[:, 512:768].indirect(T.off3[:]), F.Copy)
+    vg = V([], "copy", T.vg[:], T.idr[:].indirect(T.off3[:]))
+    wi = V([vg], "ts", T.wi[0:1, :], T.vg[0:1, :], 16, None, A.arith_shift_right)
+    ji = V([vg], "ts", T.ji[0:1, :], T.vg[0:1, :], 7, 511, A.arith_shift_right, A.bitwise_and)
+    wf = V([wi], "copy", T.wf[0:1, :], T.wi[0:1, :])
+    jf = V([ji], "copy", T.jf[0:1, :], T.ji[0:1, :])
+    outs = [dma("sync", [y0], T.y[:, c128(0)], T.yo[:, c128(0)], "dy0"), dma("sync", [y1], T.y[:, c128(1)], T.yo[:, c128(1)], "dy1"),
+            dma("sca", [y2], T.y[:, c128(2)], T.yo[:, c128(2)], "dy2"),
+            dma("sync", [wf], T["id"][0:1, :], T.wf[0:1, :], "di0"), dma("sca", [jf], T["id"][1:2, :], T.jf[0:1, :], "di1")]
+    need("pool", list(cnt.items()) + [("a1", 14), ("a2", 14), ("n1", 7), ("n2", 7), ("loc", 4 * (N - 1) + 2 * len(near)), du, dw] + dx + outs)

@@ -1,60 +1,72 @@
 from concourse.bass import DstId, RemoteDMATransfer
 from concourse.mybir import dt, AluOpType as A, ActivationFunctionType as F, AxisListType
 
-N, NB, K2, BIG = 8, 16, 32, 1.0e29
-SCRATCH = {"psb": ("psum", [128, 2048], "float32"), "pss": ("psum", [128, 2048], "float32")}
-for _d, _l in (("float8_e4m3fn_x4", "xq 512 uq 128 ur 128 wq 384 snd1 128 land1 128 snd2 32 land2 256"),
-               ("uint8", "xs 512 us 128 urs 128 ws 384 snd1s 128 land1s 128 snd2s 32 land2s 256"),
-               ("bfloat16", "xb 2048 ub 512 wb 1536 k2 96 k3 256 jb 4 g1 2560 r1 1280 g2 256 g3 1024 r3 512 oh3 512 ot3 512"),
-               ("uint16", "zoff 8 off1 8 off2 2 off3 8"), ("int32", "l2 3 i2x 2 vg 128 wi 128 ji 128"),
-               ("float32", "z32 32 zt 128 tri 128 on8 8 m8a 8 m8 8 sc1 4 st1 512 qa1 8 qb1 8 l1 8 lid 8 hid1 8 idl 32 sc2 1 st2 128 r2 128 m9 9 vp 1"
-                " oh2 96 ot2 96 p2 3 qa2 3 qb2 3 vs 1 hid2 1 vl 32 xr 256 idr 256 idc 2 tie 512 sc3 2 st3 512 qa3 8 qb3 8 l3 8 ysb 768 yo 384 wf 128 jf 128")):
+N, NB, K2, BIG, KS = 8, 16, 20, 1.0e29, 2.0 ** 80
+M = N * K2
+SCRATCH = {"psb": ("psum", [128, 2048], "float32"), "pss": ("psum", [128, 2048], "float32"),
+           "tabd": ("dram", [N, 128, 1], "float32"), "thop": ("dram", [128, 1], "float32")}
+for _d, _l in (("float8_e4m3fn_x4", "xq 512 uq 128 ur 128 wq 384 snd1 128 land1 128 snd2 32 land2 160"),
+               ("uint8", "xs 512 us 128 urs 128 ws 384 snd1s 128 land1s 128 snd2s 32 hps 20 land2s 160"),
+               ("bfloat16", "xb 2048 ub 512 wb 1536 k2 192 k3 256 jb 4 j3 2 pf 1 g1 2560 r1 1280 sg 384 sh 384 on2 256 mk2 256 g2 256 r2 256"
+                " g3 640 r3 320 oh3 512 ot3 512"),
+               ("float16", "oh2 192 ot2 192 seg 192 s2 192 sm3 257"),
+               ("uint16", "zoff 8 off1 8 kb 6 koff 16 off3 8 pk 10"), ("int32", "pi 1 si 1 bi 1 ci 1 jq 10"),
+               ("float32", "z32 32 zt 128 tri 128 ms 16 m0 16 m1 16 mk 18 sc1 4 st1 512 lt3 1 ge3 1 t1 8 u1 8 r2f 1 p8 1 key 1 t2 6 u2 6"
+                " kf 16 xr 256 kp 2 tie 320 sc3 2 st3 320 d3 8 t3 8 u3 8 ysb 480 yo 384 tab 1024 num 256 pm 1 j16 10 jj 10 jr 10 nump 160 b256 1 ido 128")):
     _w = _l.split()
     for _i in range(0, len(_w), 2):
         SCRATCH[_w[_i]] = ("sbuf", [128, int(_w[_i + 1])], _d)
-for _n, _k in (("krow", 32), ("oh1", 128), ("ot1", 128), ("sm1", 64), ("sm3", 32)):
+for _n, _k in (("krow", 32), ("oh1", 128), ("ot1", 128), ("sm1", 64)):
     SCRATCH[_n] = ("sbuf", [128, 8, _k], "bfloat16")
-SEMAPHORES = "vec sca ten pool du dx0 dx1 dx2 dx3 dw a1 a2 n1 n2 h1 h2 loc dy0 dy1 dy2 di0 di1".split()
+SCRATCH["idr"] = ("sbuf", [128, 8, 32], "float32")
+SCRATCH["kl"] = ("sbuf", [128, 8, 8], "uint16")
+SEMAPHORES = "vec sca ten pool du dx0 dx1 dx2 dx3 dw a1 a2 ak at ht hx loc dt0 dt1 dc dy0 dy1 di".split()
 
 
-def helper_of(core, T, topo):
-    c = [h for h in topo.cores_of(core) if T.rank_of(h) is None and all(topo.may_write(h, d) for d in T.cores)]
-    return sorted(c, key=lambda h: (topo.die(h) != topo.die(core), h))[0]
+def helpers(r, T, topo):
+    core = T.cores[r]
+    free = sorted((h for h in topo.cores_of(core) if T.rank_of(h) is None), key=lambda h: (topo.die(h) != topo.die(core), h))
+    wide = [h for h in free if all(topo.may_write(h, d) for d in T.cores)]
+    plain = [h for h in free if h not in wide]
+    ring = [(r + b) % N for b in range(1, N + 1)]
+    near = [d for d in ring if topo.may_write(plain[0], T.cores[d])]
+    far = [d for d in ring if d not in near]
+    return [(wide[0], "planes", far, far), (plain[0], "planes", near, near[:-1])]
 
 
-def near_engines(core, h, T, topo):
-    far = [d for d in T.cores if d != core]
-    return [e for e in topo.engines(core, h) if e not in topo.engines(core, far[0])][0:4]
-
-
-def slot2(r):
-    return 4 * (r % 2) + r // 2
-
-
-def to_all(g, core, r, first, sem, src, dst, T, topo):
+def fused(g, T, topo, sem, engines, jobs):
+    n = len(engines) // len(jobs)
     tr = []
-    for b in range(1, N):
-        d = T.cores[(r + b) % N]
+    for i, (d, src, dst) in enumerate(jobs):
         rid, pid = topo.addr(d)[0:2]
-        tr.append(RemoteDMATransfer(dst_ids=[DstId(rid=rid, pnc=pid)], dma_engine_mask=1 << topo.engines(core, d)[b - 1 + first], remote_sem=T.sem[sem], src=src(b), dst=dst))
+        tr.append(RemoteDMATransfer(dst_ids=[DstId(rid=rid, pnc=pid)], dma_engine_mask=sum(1 << e for e in engines[n * i:n * i + n]),
+                                    remote_sem=T.sem[sem], src=src, dst=dst))
     g.remote_dma_fused(tr, local_sem=T.sem.loc)
+    return n * len(jobs)
 
 
-def hand_on(g, core, r, T, topo):
-    n = len(near_engines(T.cores[r], core, T, topo))
-    g.wait_ge(T.sem.h1, n)
-    to_all(g, core, r, 0, "n1", lambda b: T.hid1[:, b:b + 1], T.idl[:, 4 * r:4 * r + 1], T, topo)
-    g.wait_ge(T.sem.h2, n)
-    to_all(g, core, r, 0, "n2", lambda b: T.hid2[:], T.vl[:, 4 * slot2(r):4 * slot2(r) + 1], T, topo)
-    g.wait_ge(T.sem.loc, 2 * (N - 1))
+def engines_of(core, T, topo):
+    off = topo.engines(core, [d for d in T.cores if topo.chip(d) != topo.chip(core) and topo.may_write(core, d)][0])
+    on = topo.engines(core, [h for h in topo.cores_of(core) if h != core][0])
+    return off, [e for e in on if e not in off]
+
+
+def hand_on(g, core, r, what, to, tab_to, T, topo):
+    off, on = engines_of(core, T, topo)
+    g.wait_ge(T.sem.ht, len(on) // 2)
+    n = fused(g, T, topo, "at", off, [(T.cores[d], T.thop[:], T.tabd[r]) for d in tab_to])
+    g.wait_ge(T.sem.hx, len(on) // 2)
+    n += fused(g, T, topo, "a2", off, [(T.cores[d], T.hps[:], T.land2s[:, K2 * r:K2 * r + K2]) for d in to])
+    g.wait_ge(T.sem.loc, n)
 
 
 def rank_program(g, core, T, topo):
     S, rank = T.sem, T.rank_of(core)
     if rank is None:
         for r in range(N):
-            if helper_of(T.cores[r], T, topo) == core:
-                hand_on(g, core, r, T, topo)
+            for h, what, to, tab_to in helpers(r, T, topo):
+                if h == core:
+                    hand_on(g, core, r, what, to, tab_to, T, topo)
         return
     q = {"vec": g.vector, "sca": g.scalar, "ten": g.tensor, "pool": g, "sync": g.sync}
     v = g.vector
@@ -102,30 +114,57 @@ def rank_program(g, core, T, topo):
     def u32(ap):
         return ap.bitcast(dt.uint32)
 
+    def u8(ap):
+        return ap.bitcast(dt.uint8)
+
     def c128(i, w=128):
         return slice(w * i, w * i + w)
 
-    du = dma("sca", [], T.ub[:], T.u[:], "du")
-    dx = [dma(("sync", "sca")[i % 2], [], T.xb[:, c128(i, 512)], T.x[:, c128(i, 512)], "dx%d" % i) for i in range(4)]
-    dw = dma("sync", [], T.wb[:], T.w[:], "dw")
+    def fold(toks, src, t, u, *last):
+        a = V(toks, "tt", t[0:64, :], src(0), src(64), A.add)
+        b = [V([a], "tt", u[p:p + 32, :], t[0:32, :], t[32:64, :], A.add) for p in (0, 32)]
+        return b, [V(b, "ts", last[0][p:p + 64, :], u[0:64, :], last[1], None, A.add) for p in (0, 64)]
 
+    du = dma("sca", [], T.ub[:, 0:8], T.u[:, 0:8], "du")
+    dx = [dma(("sync", "sca")[i % 2], [], T.xb[:, c128(i, 512)], T.x[:, c128(i, 512)], "dx%d" % i) for i in range(4)]
+    dw = dma("sync", [dx[3]], T.wb[:], T.w[:], "dw")
+
+    c_ub = V([], "set", T.ub[:, 8:512], 0.0)
     c_zoff = V([], "set", T.zoff[:], 0)
     c_zt = V([], "set", T.zt[:], 0.0)
-    c_on = V([], "set", T.on8[:], 1.0)
-    c_z32 = V([], "set", T.z32[:], 0.0)
+    V([], "set", T.ms[:], -KS)
+    c_on = V([], "set", T.on2[:], 1.0)
+    V([], "set", T.z32[:], 0.0)
+    V([], "set", T.mk[:, 8:18:9], 0.5 * KS)
+    V([], "set", T.oh3[:, 256:512], 0.0)
+    V([], "set", T.sm3[:, 0:1], 0.0)
+    t = V([], "set", T.seg[:], 1.0)
+    c_seg = V([t], "set", T.seg[:, 0:192:32], 0.0)
+    c_pi = done("pool", g.iota(T.pi[:], [[0, 1]], 0, 1))
     need("pool", [c_zt, c_on])
     c_tri = P(T.tri[:], T.zt[:], [[-1, 128]], A.is_gt, BIG, 0, 1)
     IOTA(T.jb[:], [[128, 4]], -256, 1)
     c_kr = IOTA(T.krow[:], [[1, 8], [0, 2], [8, 16]], 0, 0)
-    c_ma = P(T.m8a[:], T.on8[:], [[-16, 8]], A.is_ge, 0.0, 0, 1)
-    need("pool", [c_ma])
-    P(T.m8[:], T.m8a[:], [[16, 8]], A.is_ge, 0.0, 15, -1)
-    IOTA(T.m9[:, 8:9], [[0, 1]], 0, 1)
-    IOTA(T.k2[:, 0:64], [[16, 2], [0, 2], [1, 16]], 0, 0)
-    IOTA(T.k2[:, 64:96], [[1, 32]], 0, 0)
-    c_k3 = IOTA(T.k3[:], [[16, 8], [0, 2], [1, 16]], 0, 0)
+    P(T.mk2[:], T.on2[:], [[-1, 256]], A.not_equal, 0.0, 0, 1)
+    IOTA(T.pf[:], [[0, 1]], 0, 1)
+    c_p8 = IOTA(T.p8[:], [[0, 1]], 0, 8)
+    IOTA(T.k2[:, 128:160], [[1, 32]], 0, 0)
+    sh = K2 * rank % 32
+    IOTA(T.k2[:, 160 + sh:192], [[1, 32 - sh]], 0, 0)
+    if sh:
+        IOTA(T.k2[:, 160:160 + sh], [[1, sh]], 32 - sh, 0)
+    IOTA(T.k3[:], [[16, 8], [0, 2], [1, 16]], 0, 0)
+    for a in (0, 64):
+        IOTA(T.k2[:, a:a + 64], [[16, 2], [0, 2], [1, 16]], 0, 0)
+    IOTA(T.j3[:], [[32, 2]], 0, 1)
+    t = P(T.m0[:], T.ms[:], [[32, 2], [-K2, 8]], A.is_ge, 0.0, 0, 1)
+    IOTA(T.b256[:], [[0, 1]], 0, 256)
+    IOTA(T.j16[:], [[16, M // 16]], 0, 1)
+    need("pool", [t])
+    c_k3 = P(T.m1[:], T.m0[:], [[-32, 2], [K2, 8]], A.is_ge, 0.0, K2 - 1, -1)
+    c_tab = IOTA(T.tab[:], [[1, 8], [0, 128]], 0, 0)
 
-    t = V([du], "qz", T.uq[:], T.us[:], T.ub[:])
+    t = V([du, c_ub], "qz", T.uq[:], T.us[:], T.ub[:])
     c_ur = V([t, c_zoff], "copy", u32(T.ur[:]), u32(T.uq[:]).indirect(T.zoff[:]))
     c_us = ACT([t, c_zoff], T.urs[:], T.us[:].indirect(T.zoff[:]), F.Copy)
     U = (T.ur[:], T.urs[:])
@@ -150,120 +189,128 @@ def rank_program(g, core, T, topo):
     def count(c):
         rk[c] = V([last[c]], "scan", T.r1[:, c128(c, 320)], T.g1[:, 640 * c:640 * c + 320], T.g1[:, 640 * c + 320:640 * c + 640], 0.0, A.add, A.add)
 
+    def onehot(c):
+        oh[c] = V([rk[c], c_kr], "ts", T.oh1[:, :, c128(c, 32)], T.krow[:], T.r1[:, 320 * c + 319:320 * c + 320], T.jb[:, c:c + 1], A.is_equal, A.mult)
+
     quant(0)
     quant(1)
     blocks((0, 0), (0, 1), (1, 0), (1, 1))
     quant(2)
+    tA = MM([sc[0]], T.pss[:, 0:384], U, (T.xq[:, 0:384], T.xs[:, 0:384]))
     equal(0)
     equal(1)
     blocks((0, 2), (1, 2), (2, 0), (2, 1), (2, 2))
     quant(3)
+    sg = ACT([tA, sc[3]], T.sg[:], T.pss[:, 0:384], F.Sign, bias=T.sc1[:, 3:4], scale=-1.0)
+    t = ACT([sg], T.sh[:], T.sg[:], F.Relu, accum_out=T.lt3[:])
+    ge3 = ACT([t], T.ge3[:], T.lt3[:], F.Identity, bias=384.0, scale=-1.0)
     equal(2)
-    blocks((0, 3), (1, 3), (2, 3), (3, 0), (3, 1), (3, 2), (3, 3))
+    blocks((0, 3), (1, 3), (2, 3), (3, 3))
+    equal(3)
     for c in range(3):
         count(c)
-    equal(3)
-    count(3)
-    free1 = [last[3]] + list(sc.values())
-    for c in range(4):
-        oh[c] = V([rk[c], c_kr], "ts", T.oh1[:, :, c128(c, 32)], T.krow[:], T.r1[:, 320 * c + 319:320 * c + 320], T.jb[:, c:c + 1], A.is_equal, A.mult)
+    for c in range(3):
+        onehot(c)
+    rk[3] = V([last[3], ge3], "scan", T.r1[:, 1152:1280], T.g1[:, 2304:2432], T.g1[:, 2432:2560], T.ge3[:], A.add, A.add)
+    free1 = [last[3], sg] + list(sc.values())
+    onehot(3)
     tr = [V(list(oh.values()), "tr", T.ot1[:, b, :], T.oh1[:, b, :]) for b in range(8)]
     sm = [V([tr[b]], "scan", T.sm1[:, b, :], T.ot1[:, b, 0:64], T.ot1[:, b, 64:128], 0.0, A.add, A.add) for b in range(8)]
-
-    def fold(toks, src, qa, qb, dst):
-        t0 = V(toks, "tt", qa[0:32, :], src(0), src(32), A.add)
-        t1 = V(toks, "tt", qb[0:32, :], src(64), src(96), A.add)
-        return [V([t0, t1], "tt", dst[a:a + 32, :], qa[0:32, :], qb[0:32, :], A.add) for a in (0, 32, 64, 96)]
-
-    l1 = fold(sm, lambda a: T.sm1[a:a + 32, :, 63], T.qa1, T.qb1, T.l1)
-    off1 = V(l1, "ts", T.off1[:], T.l1[:], 256.0, None, A.add)
-    lid = ACT(l1, T.lid[:], T.l1[:], F.Identity, bias=65536.0 * rank + 32768.0, scale=128.0)
+    l1, off1 = fold(sm, lambda a: T.sm1[a:a + 64, :, 63], T.t1, T.u1, T.off1, 256.0)
     me1 = c128(rank, NB)
-    pc = V([off1], "copy", u32(T.snd1[:]), u32(T.xq[:]).indirect(T.off1[:]))
-    psc = ACT([off1], T.snd1s[:], T.xs[:].indirect(T.off1[:]), F.Copy)
+    pc = V(off1, "copy", u32(T.snd1[:]), u32(T.xq[:]).indirect(T.off1[:]))
+    psc = ACT(off1, T.snd1s[:], T.xs[:].indirect(T.off1[:]), F.Copy)
     oc = V([], "copy", u32(T.land1[:, me1]), u32(T.xq[:]).indirect(T.off1[:, 0:1]))
     osc = ACT([], T.land1s[:, me1], T.xs[:].indirect(T.off1[:, 0:1]), F.Copy)
-    oid = ACT(l1, T.idl[:, 4 * rank:4 * rank + 1], T.l1[:, 0:1], F.Identity, bias=65536.0 * rank + 32768.0, scale=128.0)
+    dt0 = dma("sync", l1, T.tabd[rank], T.u1[0:16, :], "dt0")
 
-    h = helper_of(core, T, topo)
-    hrid, hpid = topo.addr(h)[0:2]
-    near = near_engines(core, h, T, topo)
-
-    def send(tok, out, in_, sem):
-        need("pool", [tok])
-        g.remote_dma(out, in_, S[sem], S.loc, hpid, hrid, sum(1 << e for e in near))
-
-    send(lid, T.hid1[:], T.lid[:], "h1")
+    off, on = engines_of(core, T, topo)
+    hs = helpers(rank, T, topo)
+    ring = [T.cores[(rank + b) % N] for b in range(1, N)]
     need("pool", [pc])
-    to_all(g, core, rank, 0, "a1", lambda b: T.snd1[:, c128(b, NB)].bitcast(dt.uint8), T.land1[:, me1].bitcast(dt.uint8), T, topo)
+    loc = fused(g, T, topo, "a1", off[:-1], [(ring[b - 1], u8(T.snd1[:, c128(b, NB)]), u8(T.land1[:, me1])) for b in range(1, N)])
     need("pool", [psc])
-    to_all(g, core, rank, 1, "a1", lambda b: T.snd1s[:, c128(b, NB)], T.land1s[:, me1], T, topo)
+    loc += fused(g, T, topo, "a1", off[1:], [(ring[b - 1], T.snd1s[:, c128(b, NB)], T.land1s[:, me1]) for b in range(1, N)])
+    need("pool", [dt0])
+    loc += fused(g, T, topo, "ht", on, [(h[0], T.tabd[rank], T.thop[:]) for h in hs])
 
     wq = V([dw], "qz", T.wq[:], T.ws[:], T.wb[:])
+    t = V([c_pi], "ts", T.si[:], T.pi[:], 4, None, A.arith_shift_right)
+    t = V([t], "ts", T.bi[:], T.si[:], -1.0, float(rank + N), A.mult, A.add)
+    t = V([t], "ts", T.ci[:], T.bi[:], N - 1, None, A.bitwise_and)
+    c_key = V([t, c_p8], "ts", T.key[:], T.ci[:], T.p8[:], None, A.add)
+    t = V([], "ts", T.pm[:], T.si[:], -16.0, None, A.mult)
+    t = V([t, c_tab], "ts", T.jj[:], T.j16[:], T.pm[:], None, A.add)
+    t = V([t], "ts", T.jq[:], T.jj[:], 1.0 / K2, 0.5 / K2 - 0.5, A.mult, A.add)
+    t = V([t], "ts", T.jr[:], T.jq[:], float(32 - K2), None, A.mult)
+    t = V([t], "tt", T.j16[:], T.jr[:], T.jj[:], A.add)
+    c_pk = V([t], "copy", T.pk[:], T.j16[:])
 
     arr1 = [("a1", 14), oc, osc]
     L1 = (T.land1[:], T.land1s[:])
     t = MM(arr1 + free1, T.pss[:, 0:128], L1, U)
     tB2 = MM([], T.psb[:, 0:128], U, L1)
-    sc2 = ACT([t], T.sc2[:], T.pss[:, 0:1], F.Copy)
-    st2 = ACT([sc2], T.st2[:], T.tri[:], F.Identity, bias=T.sc2[:])
-    V([tB2, sc2], "ts", T.g2[:, 0:128], T.psb[:, 0:128], T.sc2[:], None, A.is_gt)
-    e2 = V([st2], "tt", T.g2[:, 128:256], T.psb[:, 0:128], T.st2[:], A.is_equal)
-    t = V([("n1", 7), oid, c_k3], "tt", T.m9[:, 0:8], T.idl[:, 0:32:4], T.m8[:], A.mult)
-    r2 = V([e2], "scan", T.r2[:], T.g2[:, 0:128], T.g2[:, 128:256], 0.0, A.add, A.add)
-    vp = V([t], "red", T.vp[:], T.m9[:], AxisListType.X, A.add)
-    t = V([r2, vp], "ts", T.oh2[:], T.k2[:], T.r2[:, 127:128], T.vp[:], A.is_equal, A.mult)
+    V([tB2, c_k3], "ts", T.g2[:, 0:128], T.psb[:, 0:128], T.pss[:, 0:1], -1.0, A.is_equal, A.mult)
+    e2 = V([], "ts", T.g2[:, 128:256], T.psb[:, 0:128], T.pss[:, 0:1], None, A.is_ge)
+    r2 = V([e2], "scan", T.r2[:], T.mk2[:], T.g2[:], 0.0, A.mult, A.add)
+    t = V([r2], "copy", T.r2f[:], T.r2[:, 255:256])
+    V([], "ts", T.oh2[:, 0:64], T.k2[:, 0:64], T.r2[:, 255:256], T.pf[:], A.is_equal, A.mult)
+    t = V([t, c_key], "ts", T.oh2[:, 64:192], T.k2[:, 64:192], T.r2f[:], T.key[:], A.is_equal, A.mult)
     t = V([t], "tr", T.ot2[:], T.oh2[:])
-    p2 = [V([t], "red", T.p2[:, b:b + 1], T.ot2[:, c128(b, 32)], AxisListType.X, A.add) for b in range(3)]
-    l2 = fold(p2, lambda a: T.p2[a:a + 32, :], T.qa2, T.qb2, T.l2)
-    t = V(l2, "ts", T.i2x[:], T.l2[:, 0:2], 127, None, A.bitwise_and)
-    vs = V(l2, "copy", T.vs[:], T.l2[:, 2:3])
-    off2 = V([t], "copy", T.off2[:], T.i2x[:])
-    b2 = slot2(rank)
-    me2 = c128(b2, K2)
-    pc = V([off2] + arr1, "copy", u32(T.snd2[:]), u32(T.land1[:]).indirect(T.off2[:]))
-    psc = ACT([off2] + arr1, T.snd2s[:], T.land1s[:].indirect(T.off2[:]), F.Copy)
-    oc2 = V([], "copy", u32(T.land2[:, me2]), u32(T.land1[:]).indirect(T.off2[:]))
-    osc2 = ACT([], T.land2s[:, me2], T.land1s[:].indirect(T.off2[:]), F.Copy)
-    ov = V(l2, "copy", T.vl[:, 4 * b2:4 * b2 + 1], T.l2[:, 2:3])
-    send(vs, T.hid2[:], T.vs[:], "h2")
-    need("pool", [pc])
-    to_all(g, core, rank, 0, "a2", lambda b: T.snd2[:].bitcast(dt.uint8), T.land2[:, me2].bitcast(dt.uint8), T, topo)
+    t = V([t, c_seg], "scan", T.s2[:], T.seg[:], T.ot2[:], 0.0, A.mult, A.add)
+    off2 = fold([t], lambda a: T.s2[a:a + 64, 31:192:32], T.t2, T.u2, T.kb, 0.0)[1]
+    me2 = c128(rank, K2)
+    pc = V(off2 + arr1, "copy", u32(T.snd2[:]), u32(T.land1[:]).indirect(T.kb[:, 0:2]))
+    psc = ACT(off2 + arr1, T.snd2s[:], T.land1s[:].indirect(T.kb[:, 0:2]), F.Copy)
+    need("pool", off2)
+    loc += fused(g, T, topo, "ak", off[1:], [(d, T.kb[:, 2:6], T.kl[:, rank, 0:4]) for d in ring])
+    ok = V([], "copy", T.kl[:, rank, 0:4], T.kb[:, 2:6])
     need("pool", [psc])
-    to_all(g, core, rank, 1, "a2", lambda b: T.snd2s[:], T.land2s[:, me2], T, topo)
+    loc += fused(g, T, topo, "hx", on, [(h[0], T.snd2s[:, 0:K2], T.hps[:]) for h in hs if h[1] == "planes"])
+    need("pool", [pc])
+    loc += fused(g, T, topo, "a2", off[:-1], [(d, u8(T.snd2[:, 0:K2]), u8(T.land2[:, me2])) for d in ring])
+    dc = dma("sync", [pc], u8(T.land2[:, me2]), u8(T.snd2[:, 0:K2]), "dc")
+    at = ("at", sum(len(off) // len(h[3]) for r in range(N) for h in helpers(r, T, topo) if rank in h[3]))
+    dt1 = dma("sync", [at, dt0, c_tab], T.tab[1:2, :], T.tabd[:], "dt1")
 
-    xr = [ACT([("n2", 7), ov, c_z32], T.xr[:, c128(b, 32)], T.z32[:], F.Identity, bias=T.vl[:, 4 * b:4 * b + 1]) for b in range(8)]
-    idc = [V([("n2", 7), ov], "copy", T.idc[32 * a:32 * a + 32, :], T.vl[32 * a:32 * a + 32, 4 * a:32:16]) for a in range(4)]
+    ak = ("ak", N - 1)
+    kf = V([ak, ok], "copy", T.kf[:], T.kl[:, :, 2:4])
+    xr = [ACT([kf], T.xr[:, c128(b, 32)], T.z32[:], F.Identity, bias=T.kf[:, 2 * b:2 * b + 1]) for b in range(8)]
+    t = [V([kf], "tt", T.mk[:, 9 * c:9 * c + 8], T.kf[:, 1:16:2], T.m1[:, c128(c, 8)], A.mult) for c in range(2)]
+    kp = [V([t[c]], "red", T.kp[:, c:c + 1], T.mk[:, c128(c, 9)], AxisListType.X, A.add) for c in range(2)]
+    koff = [V([], "copy", T.koff[:], T.kl[:, :, 0:2])]
     idr = V(xr, "tr", T.idr[:], T.xr[:])
-    tie = [V([idr] + idc, "ts", T.tie[:, c128(c, 256)], T.idr[:], T.idc[:, c:c + 1], BIG, A.is_ge, A.mult) for c in range(2)]
+    lanes = (slice(0, 128), slice(96, 128))
+    tie = [ACT([idr] + kp, T.tie[lanes[c], c128(c, M)], T.idr[lanes[c], :, 0:K2], F.Relu, bias=T.kp[lanes[c], c:c + 1], scale=KS) for c in range(2)]
 
-    arr2 = [("a2", 14), oc2, osc2]
+    arr2 = [("a2", N - 1 + 2 * N), dc]
     L2 = (T.land2[:], T.land2s[:])
-    tS3 = [MM(arr2 + [e2, sc2] + free1, T.pss[:, 512 * c + 512:512 * c + 640], (T.land2[:, c128(c)], T.land2s[:, c128(c)]), U) for c in range(2)]
-    b3 = T.psb[:, 512:768]
-    tB3 = MM([], b3, U, L2)
-    yps = [T.psb[:, 1024:1280], T.psb[:, 1536:1792], T.pss[:, 1536:1792]]
+    tS3 = [MM(arr2 + [e2] + free1, T.pss[:, 512 * c + 512:512 * c + 640], (T.land2[:, 32 * c:32 * c + 128], T.land2s[:, 32 * c:32 * c + 128]), U) for c in range(2)]
+    tB3 = MM([], T.psb[:, 512:512 + M], U, L2)
+    yps = [T.psb[:, 1024:1024 + M], T.psb[:, 1536:1536 + M], T.pss[:, 1536:1536 + M]]
     tY = [MM([wq], yps[o], (T.wq[:, c128(o)], T.ws[:, c128(o)]), L2) for o in range(3)]
-    sc3 = [ACT([tS3[c]], T.sc3[:, c:c + 1], T.pss[:, 512 * c + 512:512 * c + 513], F.Copy) for c in range(2)]
-    st3 = [ACT([sc3[c], tie[c]], T.st3[:, c128(c, 256)], T.tie[:, c128(c, 256)], F.Identity, bias=T.sc3[:, c:c + 1]) for c in range(2)]
-    ysb = [ACT([tY[o]], T.ysb[:, c128(o, 256)], yps[o], F.Copy) for o in range(3)]
-    g3 = [V([tB3, sc3[c]], "ts", T.g3[:, 512 * c:512 * c + 256], b3, T.sc3[:, c:c + 1], None, A.is_gt) for c in range(2)]
-    e3 = [V([st3[c]], "tt", T.g3[:, 512 * c + 256:512 * c + 512], b3, T.st3[:, c128(c, 256)], A.is_equal) for c in range(2)]
-    r3 = [V([g3[c], e3[c]], "scan", T.r3[:, c128(c, 256)], T.g3[:, 512 * c:512 * c + 256], T.g3[:, 512 * c + 256:512 * c + 512], 0.0, A.add, A.add) for c in range(2)]
-    oh3 = [V([r3[c]], "ts", T.oh3[:, c128(c, 256)], T.k3[:], T.r3[:, 256 * c + 255:256 * c + 256], T.jb[:, c + 2:c + 3], A.is_equal, A.mult) for c in range(2)]
-    t = V(oh3, "tr", T.ot3[:], T.oh3[:])
-    sm3 = [V([t], "scan", T.sm3[:, b, :], T.ot3[:, c128(b, 32)], T.ot3[:, 256 + 32 * b:288 + 32 * b], 0.0, A.add, A.add) for b in range(8)]
-    l3 = fold(sm3, lambda a: T.sm3[a:a + 32, :, 31], T.qa3, T.qb3, T.l3)
-    off3 = V(l3, "copy", T.off3[:], T.l3[:])
-    y0 = V([off3] + ysb, "copy", T.yo[:, c128(0)], T.ysb[:, 0:256].indirect(T.off3[:]))
-    y1 = ACT([off3] + ysb, T.yo[:, c128(1)], T.ysb[:, 256:512].indirect(T.off3[:]), F.Copy)
-    y2 = ACT([], T.yo[:, c128(2)], T.ysb[:, 512:768].indirect(T.off3[:]), F.Copy)
-    vg = V([], "copy", T.vg[:], T.idr[:].indirect(T.off3[:]))
-    wi = V([vg], "ts", T.wi[0:1, :], T.vg[0:1, :], 16, None, A.arith_shift_right)
-    ji = V([vg], "ts", T.ji[0:1, :], T.vg[0:1, :], 7, 511, A.arith_shift_right, A.bitwise_and)
-    wf = V([wi], "copy", T.wf[0:1, :], T.wi[0:1, :])
-    jf = V([ji], "copy", T.jf[0:1, :], T.ji[0:1, :])
-    outs = [dma("sync", [y0], T.y[:, c128(0)], T.yo[:, c128(0)], "dy0"), dma("sync", [y1], T.y[:, c128(1)], T.yo[:, c128(1)], "dy1"),
-            dma("sca", [y2], T.y[:, c128(2)], T.yo[:, c128(2)], "dy2"),
-            dma("sync", [wf], T["id"][0:1, :], T.wf[0:1, :], "di0"), dma("sca", [jf], T["id"][1:2, :], T.jf[0:1, :], "di1")]
-    need("pool", list(cnt.items()) + [("a1", 14), ("a2", 14), ("n1", 7), ("n2", 7), ("loc", 4 * (N - 1) + 2 * len(near)), du, dw] + dx + outs)
+    sc3 = ACT(tS3, T.sc3[:], T.pss[:, 512:1025:512], F.Copy)
+    st3 = [ACT([sc3, tie[c]], T.st3[lanes[c], c128(c, M)], T.tie[lanes[c], c128(c, M)], F.Identity, bias=T.sc3[lanes[c], c:c + 1]) for c in range(2)]
+    ysb = [ACT([tY[o]], T.ysb[:, c128(o, M)], yps[o], F.Copy) for o in range(3)]
+    t = ACT(koff + [dt1], T.num[:], T.tab[:].indirect(T.koff[:]), F.Copy)
+    nump = ACT([t, c_pk], T.nump[:], T.num[:].indirect(T.pk[:]), F.Copy)
+    g3, e3, r3, oh3 = {}, {}, {}, {}
+    for c in range(2):
+        g3[c] = V([tB3, sc3], "ts", T.g3[lanes[c], c128(2 * c, M)], T.psb[lanes[c], 512:512 + M], T.sc3[lanes[c], c:c + 1], None, A.is_gt)
+    for c in range(2):
+        e3[c] = V([st3[c]], "tt", T.g3[lanes[c], c128(2 * c + 1, M)], T.psb[lanes[c], 512:512 + M], T.st3[lanes[c], c128(c, M)], A.is_equal)
+    for c in range(2):
+        r3[c] = V([g3[c], e3[c]], "scan", T.r3[lanes[c], c128(c, M)], T.g3[lanes[c], c128(2 * c, M)], T.g3[lanes[c], c128(2 * c + 1, M)], 0.0, A.add, A.add)
+    for c in range(2):
+        oh3[c] = V([r3[c]], "ts", T.oh3[lanes[c], c128(c, 256)], T.k3[lanes[c], :], T.r3[lanes[c], M * c + M - 1:M * c + M], T.j3[lanes[c], c:c + 1], A.is_equal, A.mult)
+    t = V(list(oh3.values()), "tr", T.ot3[:], T.oh3[:])
+    t = V([t], "scan", T.sm3[:, 1:257], T.ot3[:, 0:256], T.ot3[:, 256:512], 0.0, A.add, A.add)
+    t = V([t], "tt", T.d3[:], T.sm3[:, 32:257:32], T.sm3[:, 0:256:32], A.subtract)
+    off3 = fold([t], lambda a: T.d3[a:a + 64, :], T.t3, T.u3, T.off3, 0.0)[1]
+    y0 = V(off3 + ysb, "copy", T.yo[:, c128(0)], T.ysb[:, c128(0, M)].indirect(T.off3[:]))
+    y1 = ACT(off3 + ysb, T.yo[:, c128(1)], T.ysb[:, c128(1, M)].indirect(T.off3[:]), F.Copy)
+    y2 = V([], "copy", T.yo[:, c128(2)], T.ysb[:, c128(2, M)].indirect(T.off3[:]))
+    ido = ACT([nump], T.ido[:], T.nump[:].indirect(T.off3[:]), F.Identity, bias=T.b256[:])
+    outs = [dma("sync", [y0, y1], T.y[:, 0:256], T.yo[:, 0:256], "dy0"), dma("sync", [y2], T.y[:, c128(2)], T.yo[:, c128(2)], "dy1"),
+            dma("sca", [ido], T["id"][:], T.ido[0:2, :], "di")]
+    need("pool", list(cnt.items()) + arr1 + arr2 + [ak, at, dt1, ("loc", loc), du, dw] + dx + outs)

@@ -1,26 +1,29 @@
 from concourse.bass import DstId, RemoteDMATransfer
 from concourse.mybir import dt, AluOpType as A, ActivationFunctionType as F, AxisListType
 
-N, NB, K2, BIG, KS = 8, 16, 20, 1.0e29, 2.0 ** 80
+N, NB, K2, KS = 8, 16, 20, 2.0 ** 80
+STEP, TINY = 0.625 * 2.0 ** -23, 2.0 ** -124
 M = N * K2
 SCRATCH = {"psb": ("psum", [128, 2048], "float32"), "pss": ("psum", [128, 2048], "float32"),
            "tabd": ("dram", [N, 128, 1], "float32"), "thop": ("dram", [128, 1], "float32")}
-for _d, _l in (("float8_e4m3fn_x4", "xq 512 uq 128 ur 128 wq 384 snd1 128 land1 128 snd2 32 land2 160"),
+for _d, _l in (("float8_e4m3fn_x4", "xq 512 uq 128 ur 128 wq 384 snd1 128 land1 128 snd2 32 hq 20 land2 160"),
                ("uint8", "xs 512 us 128 urs 128 ws 384 snd1s 128 land1s 128 snd2s 32 hps 20 land2s 160"),
-               ("bfloat16", "xb 2048 ub 512 wb 1536 k2 192 k3 256 jb 4 j3 2 pf 1 g1 2560 r1 1280 sg 384 sh 384 on2 256 mk2 256 g2 256 r2 256"
+               ("bfloat16", "xb 2048 ub 512 wb 1536 k2 192 k3 256 jb 4 j3 2 pf 1 g1 2048 r1 1024 on2 256 mk2 256 g2 256 r2 256"
                 " g3 640 r3 320 oh3 512 ot3 512"),
                ("float16", "oh2 192 ot2 192 seg 192 s2 192 sm3 257"),
                ("uint16", "zoff 8 off1 8 kb 6 koff 16 off3 8 pk 10"), ("int32", "pi 1 si 1 bi 1 ci 1 jq 10"),
-               ("float32", "z32 32 zt 128 tri 128 ms 16 m0 16 m1 16 mk 18 sc1 4 st1 512 lt3 1 ge3 1 t1 8 u1 8 r2f 1 p8 1 key 1 t2 6 u2 6"
+               ("float32", "z32 32 zt 128 tri 128 ms 16 m0 16 m1 16 mk 18 sc1 4 st1 512 up1 4 ge1 4 u1 8 r2f 1 p8 1 key 1 t2 6 u2 6"
                 " kf 16 xr 256 kp 2 tie 320 sc3 2 st3 320 d3 8 t3 8 u3 8 ysb 480 yo 384 tab 1024 num 256 pm 1 j16 10 jj 10 jr 10 nump 160 b256 1 ido 128")):
     _w = _l.split()
     for _i in range(0, len(_w), 2):
         SCRATCH[_w[_i]] = ("sbuf", [128, int(_w[_i + 1])], _d)
-for _n, _k in (("krow", 32), ("oh1", 128), ("ot1", 128), ("sm1", 64)):
+for _n, _k in (("krow1", 32), ("krow2", 32), ("krow3", 32), ("oh1", 128), ("ot1", 128), ("sm1", 128)):
     SCRATCH[_n] = ("sbuf", [128, 8, _k], "bfloat16")
+for _n in ("sg", "sh"):
+    SCRATCH[_n] = ("sbuf", [128, 2, 384], "bfloat16")
 SCRATCH["idr"] = ("sbuf", [128, 8, 32], "float32")
 SCRATCH["kl"] = ("sbuf", [128, 8, 8], "uint16")
-SEMAPHORES = "vec sca ten pool du dx0 dx1 dx2 dx3 dw a1 a2 ak at ht hx loc dt0 dt1 dc dy0 dy1 di".split()
+SEMAPHORES = "vec sca ten pool du dx0 dx1 dx2 dx3 dw a1 a2 ak at ht hx loc dt0 dt1 dy0 dy1 di".split()
 
 
 def helpers(r, T, topo):
@@ -31,18 +34,19 @@ def helpers(r, T, topo):
     ring = [(r + b) % N for b in range(1, N + 1)]
     near = [d for d in ring if topo.may_write(plain[0], T.cores[d])]
     far = [d for d in ring if d not in near]
-    return [(wide[0], "planes", far, far), (plain[0], "planes", near, near[:-1])]
+    return [(wide[0], "planes", far, far), (plain[0], "planes", near, near[:2]), (plain[1], "codes", near, near[2:-1])]
 
 
-def fused(g, T, topo, sem, engines, jobs):
-    n = len(engines) // len(jobs)
+def fused(g, T, topo, sem, engines, jobs, share=None):
+    share = share or [len(engines) // len(jobs)] * len(jobs)
     tr = []
     for i, (d, src, dst) in enumerate(jobs):
         rid, pid = topo.addr(d)[0:2]
-        tr.append(RemoteDMATransfer(dst_ids=[DstId(rid=rid, pnc=pid)], dma_engine_mask=sum(1 << e for e in engines[n * i:n * i + n]),
+        mine = engines[sum(share[:i]):sum(share[:i + 1])]
+        tr.append(RemoteDMATransfer(dst_ids=[DstId(rid=rid, pnc=pid)], dma_engine_mask=sum(1 << e for e in mine),
                                     remote_sem=T.sem[sem], src=src, dst=dst))
     g.remote_dma_fused(tr, local_sem=T.sem.loc)
-    return n * len(jobs)
+    return sum(share)
 
 
 def engines_of(core, T, topo):
@@ -53,10 +57,14 @@ def engines_of(core, T, topo):
 
 def hand_on(g, core, r, what, to, tab_to, T, topo):
     off, on = engines_of(core, T, topo)
-    g.wait_ge(T.sem.ht, len(on) // 2)
+    g.wait_ge(T.sem.ht, len(on) // 4)
     n = fused(g, T, topo, "at", off, [(T.cores[d], T.thop[:], T.tabd[r]) for d in tab_to])
-    g.wait_ge(T.sem.hx, len(on) // 2)
-    n += fused(g, T, topo, "a2", off, [(T.cores[d], T.hps[:], T.land2s[:, K2 * r:K2 * r + K2]) for d in to])
+    g.wait_ge(T.sem.hx, len(on) // (2 if what == "planes" else 1))
+    if what == "planes":
+        src, dst = T.hps[:, 0:K2], T.land2s[:, K2 * r:K2 * r + K2]
+    else:
+        src, dst = T.hq[:].bitcast(dt.uint8), T.land2[:, K2 * r:K2 * r + K2].bitcast(dt.uint8)
+    n += fused(g, T, topo, "a2", off, [(T.cores[d], src, dst) for d in to])
     g.wait_ge(T.sem.loc, n)
 
 
@@ -121,12 +129,15 @@ def rank_program(g, core, T, topo):
         return slice(w * i, w * i + w)
 
     def fold(toks, src, t, u, *last):
-        a = V(toks, "tt", t[0:64, :], src(0), src(64), A.add)
-        b = [V([a], "tt", u[p:p + 32, :], t[0:32, :], t[32:64, :], A.add) for p in (0, 32)]
+        if t is None:
+            b = [V(toks, "tt", u[p:p + 32, :], src(0), src(32), A.add) for p in (0, 32)]
+        else:
+            a = V(toks, "tt", t[0:64, :], src(0), src(64), A.add)
+            b = [V([a], "tt", u[p:p + 32, :], t[0:32, :], t[32:64, :], A.add) for p in (0, 32)]
         return b, [V(b, "ts", last[0][p:p + 64, :], u[0:64, :], last[1], None, A.add) for p in (0, 64)]
 
     du = dma("sca", [], T.ub[:, 0:8], T.u[:, 0:8], "du")
-    dx = [dma(("sync", "sca")[i % 2], [], T.xb[:, c128(i, 512)], T.x[:, c128(i, 512)], "dx%d" % i) for i in range(4)]
+    dx = [dma("sync", [], T.xb[:, c128(i, 512)], T.x[:, c128(i, 512)], "dx%d" % i) for i in range(4)]
     dw = dma("sync", [dx[3]], T.wb[:], T.w[:], "dw")
 
     c_ub = V([], "set", T.ub[:, 8:512], 0.0)
@@ -142,9 +153,11 @@ def rank_program(g, core, T, topo):
     c_seg = V([t], "set", T.seg[:, 0:192:32], 0.0)
     c_pi = done("pool", g.iota(T.pi[:], [[0, 1]], 0, 1))
     need("pool", [c_zt, c_on])
-    c_tri = P(T.tri[:], T.zt[:], [[-1, 128]], A.is_gt, BIG, 0, 1)
+    c_tri = P(T.tri[:], T.zt[:], [[-1, 128]], A.is_gt, 1.0, 0, 1)
     IOTA(T.jb[:], [[128, 4]], -256, 1)
-    c_kr = IOTA(T.krow[:], [[1, 8], [0, 2], [8, 16]], 0, 0)
+    IOTA(T.krow1[:], [[1, 8], [0, 2], [8, 16]], 0, 0)
+    IOTA(T.krow2[:], [[2, 8], [0, 2], [16, 16]], -256, 0)
+    c_kr = IOTA(T.krow3[:], [[2, 8], [0, 2], [16, 16]], -384, 0)
     P(T.mk2[:], T.on2[:], [[-1, 256]], A.not_equal, 0.0, 0, 1)
     IOTA(T.pf[:], [[0, 1]], 0, 1)
     c_p8 = IOTA(T.p8[:], [[0, 1]], 0, 8)
@@ -153,23 +166,16 @@ def rank_program(g, core, T, topo):
     IOTA(T.k2[:, 160 + sh:192], [[1, 32 - sh]], 0, 0)
     if sh:
         IOTA(T.k2[:, 160:160 + sh], [[1, sh]], 32 - sh, 0)
-    IOTA(T.k3[:], [[16, 8], [0, 2], [1, 16]], 0, 0)
     for a in (0, 64):
         IOTA(T.k2[:, a:a + 64], [[16, 2], [0, 2], [1, 16]], 0, 0)
-    IOTA(T.j3[:], [[32, 2]], 0, 1)
-    t = P(T.m0[:], T.ms[:], [[32, 2], [-K2, 8]], A.is_ge, 0.0, 0, 1)
-    IOTA(T.b256[:], [[0, 1]], 0, 256)
-    IOTA(T.j16[:], [[16, M // 16]], 0, 1)
-    need("pool", [t])
-    c_k3 = P(T.m1[:], T.m0[:], [[-32, 2], [K2, 8]], A.is_ge, 0.0, K2 - 1, -1)
-    c_tab = IOTA(T.tab[:], [[1, 8], [0, 128]], 0, 0)
+    c_k2 = IOTA(T.j16[:], [[16, M // 16]], 0, 1)
 
     t = V([du, c_ub], "qz", T.uq[:], T.us[:], T.ub[:])
     c_ur = V([t, c_zoff], "copy", u32(T.ur[:]), u32(T.uq[:]).indirect(T.zoff[:]))
     c_us = ACT([t, c_zoff], T.urs[:], T.us[:].indirect(T.zoff[:]), F.Copy)
     U = (T.ur[:], T.urs[:])
 
-    tq, tB, sc, st, rk, oh, last = {}, {}, {}, {}, {}, {}, {}
+    tq, tA, tB, sc, up, sg, ge, st, rk, oh, last = [{} for _ in range(11)]
 
     def quant(i):
         X = (T.xq[:, c128(i)], T.xs[:, c128(i)])
@@ -177,46 +183,60 @@ def rank_program(g, core, T, topo):
         t = MM([tq[i], c_ur, c_us], T.pss[:, 512 * i:512 * i + 128], X, U)
         tB[i] = MM([], T.psb[:, 512 * i:512 * i + 128], U, X)
         sc[i] = ACT([t], T.sc1[:, i:i + 1], T.pss[:, 512 * i:512 * i + 1], F.Copy)
-        st[i] = ACT([sc[i], c_tri], T.st1[:, c128(i)], T.tri[:], F.Identity, bias=T.sc1[:, i:i + 1])
+        up[i] = ACT([], T.up1[:, i:i + 1], T.pss[:, 512 * i:512 * i + 1], F.Abs, bias=TINY, scale=STEP)
+        if i in (1, 2):
+            tA[i + 1] = MM([up[i - 1]], T.pss[:, 512 * i - 512:640 * i - 384], U, (T.xq[:, 0:128 * i + 128], T.xs[:, 0:128 * i + 128]))
+        if i >= 2:
+            sg[i] = ACT([tA[i], sc[i]], T.sg[:, i - 2, 0:128 * i], T.pss[:, 512 * i - 1024:640 * i - 1024], F.Sign, bias=T.sc1[:, i:i + 1], scale=-1.0)
+        st[i] = ACT([up[i], c_tri], T.st1[:, c128(i)], T.tri[:], F.Identity, bias=T.sc1[:, i:i + 1], scale=T.up1[:, i:i + 1])
+        if i >= 2:
+            ge[i] = ACT([sg[i]], T.sh[:, i - 2, 0:128 * i], T.sg[:, i - 2, 0:128 * i], F.Sign, bias=0.5, scale=-1.0, accum_out=T.ge1[:, i:i + 1])
 
     def blocks(*ci):
         for c, i in ci:
-            last[c] = V([tB[i], sc[c]], "ts", T.g1[:, 640 * c + 128 * i:640 * c + 128 * i + 128], T.psb[:, 512 * i:512 * i + 128], T.sc1[:, c:c + 1], None, A.is_ge if i < c else A.is_gt)
-
-    def equal(c):
-        last[c] = V([tB[c], st[c]], "tt", T.g1[:, 640 * c + 512:640 * c + 640], T.psb[:, 512 * c:512 * c + 128], T.st1[:, c128(c)], A.is_equal)
+            out, s = T.g1[:, 512 * c + 128 * i:512 * c + 128 * i + 128], T.psb[:, 512 * i:512 * i + 128]
+            if i == c:
+                last[c] = V([tB[c], st[c]], "tt", out, s, T.st1[:, c128(c)], A.is_ge)
+            else:
+                last[c] = V([tB[i], sc[c]], "ts", out, s, T.sc1[:, c:c + 1], None, A.is_ge if i < c else A.is_gt)
 
     def count(c):
-        rk[c] = V([last[c]], "scan", T.r1[:, c128(c, 320)], T.g1[:, 640 * c:640 * c + 320], T.g1[:, 640 * c + 320:640 * c + 640], 0.0, A.add, A.add)
+        if c < 2:
+            rk[c] = V([last[c]], "scan", T.r1[:, c128(c, 256)], T.g1[:, 512 * c:512 * c + 256], T.g1[:, 512 * c + 256:512 * c + 512], 0.0, A.add, A.add)
+        else:
+            own = T.g1[:, 640 * c:512 * c + 512]
+            rk[c] = V([last[c], ge[c]], "scan", T.r1[:, 384 * c - 256:256 * c + 256], own, own, T.ge1[:, c:c + 1], A.add, A.add)
 
     def onehot(c):
-        oh[c] = V([rk[c], c_kr], "ts", T.oh1[:, :, c128(c, 32)], T.krow[:], T.r1[:, 320 * c + 319:320 * c + 320], T.jb[:, c:c + 1], A.is_equal, A.mult)
+        oh[c] = V([rk[c], c_kr], "ts", T.oh1[:, :, c128(c, 32)], T["krow%d" % max(c, 1)][:], T.r1[:, 256 * c + 255:256 * c + 256], T.jb[:, c:c + 1], A.is_equal, A.mult)
 
+    def turn(c):
+        tr[c] = V([oh[c]], "tr", T.ot1[:, :, c128(c, 32)], T.oh1[:, :, c128(c, 32)])
+
+    tr = {}
     quant(0)
     quant(1)
-    blocks((0, 0), (0, 1), (1, 0), (1, 1))
     quant(2)
-    tA = MM([sc[0]], T.pss[:, 0:384], U, (T.xq[:, 0:384], T.xs[:, 0:384]))
-    equal(0)
-    equal(1)
-    blocks((0, 2), (1, 2), (2, 0), (2, 1), (2, 2))
+    blocks((0, 1), (1, 0))
     quant(3)
-    sg = ACT([tA, sc[3]], T.sg[:], T.pss[:, 0:384], F.Sign, bias=T.sc1[:, 3:4], scale=-1.0)
-    t = ACT([sg], T.sh[:], T.sg[:], F.Relu, accum_out=T.lt3[:])
-    ge3 = ACT([t], T.ge3[:], T.lt3[:], F.Identity, bias=384.0, scale=-1.0)
-    equal(2)
-    blocks((0, 3), (1, 3), (2, 3), (3, 3))
-    equal(3)
-    for c in range(3):
-        count(c)
-    for c in range(3):
-        onehot(c)
-    rk[3] = V([last[3], ge3], "scan", T.r1[:, 1152:1280], T.g1[:, 2304:2432], T.g1[:, 2432:2560], T.ge3[:], A.add, A.add)
-    free1 = [last[3], sg] + list(sc.values())
+    blocks((0, 0), (0, 2), (1, 2), (1, 1), (0, 3), (1, 3))
+    count(0)
+    count(1)
+    blocks((2, 3), (2, 2))
+    onehot(0)
+    onehot(1)
+    count(2)
+    turn(0)
+    blocks((3, 3))
+    onehot(2)
+    turn(1)
+    count(3)
+    turn(2)
     onehot(3)
-    tr = [V(list(oh.values()), "tr", T.ot1[:, b, :], T.oh1[:, b, :]) for b in range(8)]
-    sm = [V([tr[b]], "scan", T.sm1[:, b, :], T.ot1[:, b, 0:64], T.ot1[:, b, 64:128], 0.0, A.add, A.add) for b in range(8)]
-    l1, off1 = fold(sm, lambda a: T.sm1[a:a + 64, :, 63], T.t1, T.u1, T.off1, 256.0)
+    turn(3)
+    free1 = [last[3], sg[3]]
+    sm = [V([tr[3]], "scan", T.sm1[0:64, b, :], T.ot1[0:64, b, :], T.ot1[64:128, b, :], 0.0, A.add, A.add) for b in range(8)]
+    l1, off1 = fold(sm, lambda a: T.sm1[a:a + 32, :, 127], None, T.u1, T.off1, 256.0)
     me1 = c128(rank, NB)
     pc = V(off1, "copy", u32(T.snd1[:]), u32(T.xq[:]).indirect(T.off1[:]))
     psc = ACT(off1, T.snd1s[:], T.xs[:].indirect(T.off1[:]), F.Copy)
@@ -228,9 +248,20 @@ def rank_program(g, core, T, topo):
     hs = helpers(rank, T, topo)
     ring = [T.cores[(rank + b) % N] for b in range(1, N)]
     need("pool", [pc])
-    loc = fused(g, T, topo, "a1", off[:-1], [(ring[b - 1], u8(T.snd1[:, c128(b, NB)]), u8(T.land1[:, me1])) for b in range(1, N)])
+    codes = [(ring[b - 1], u8(T.snd1[:, c128(b, NB)]), u8(T.land1[:, me1])) for b in range(1, N)]
+    planes = [(ring[b - 1], T.snd1s[:, c128(b, NB)], T.land1s[:, me1]) for b in range(1, N)]
+    loc = fused(g, T, topo, "a1", off, codes[0::2])
     need("pool", [psc])
-    loc += fused(g, T, topo, "a1", off[1:], [(ring[b - 1], T.snd1s[:, c128(b, NB)], T.land1s[:, me1]) for b in range(1, N)])
+    loc += fused(g, T, topo, "a1", off, planes[0::2])
+    loc += fused(g, T, topo, "a1", off, codes[1::2], (4, 2, 2))
+    loc += fused(g, T, topo, "a1", off, planes[1::2], (2, 2, 4))
+    loc1 = loc
+    t = P(T.m0[:], T.ms[:], [[32, 2], [-K2, 8]], A.is_ge, 0.0, 0, 1)
+    IOTA(T.k3[:], [[16, 8], [0, 2], [1, 16]], 0, 0)
+    IOTA(T.j3[:], [[32, 2]], 0, 1)
+    IOTA(T.b256[:], [[0, 1]], 0, 256)
+    need("pool", [t])
+    c_k3 = P(T.m1[:], T.m0[:], [[-32, 2], [K2, 8]], A.is_ge, 0.0, K2 - 1, -1)
     need("pool", [dt0])
     loc += fused(g, T, topo, "ht", on, [(h[0], T.tabd[rank], T.thop[:]) for h in hs])
 
@@ -240,17 +271,18 @@ def rank_program(g, core, T, topo):
     t = V([t], "ts", T.ci[:], T.bi[:], N - 1, None, A.bitwise_and)
     c_key = V([t, c_p8], "ts", T.key[:], T.ci[:], T.p8[:], None, A.add)
     t = V([], "ts", T.pm[:], T.si[:], -16.0, None, A.mult)
-    t = V([t, c_tab], "ts", T.jj[:], T.j16[:], T.pm[:], None, A.add)
+    t = V([t, c_k2], "ts", T.jj[:], T.j16[:], T.pm[:], None, A.add)
     t = V([t], "ts", T.jq[:], T.jj[:], 1.0 / K2, 0.5 / K2 - 0.5, A.mult, A.add)
     t = V([t], "ts", T.jr[:], T.jq[:], float(32 - K2), None, A.mult)
     t = V([t], "tt", T.j16[:], T.jr[:], T.jj[:], A.add)
     c_pk = V([t], "copy", T.pk[:], T.j16[:])
+    c_tab = [V([], "set", T.tab[:, c128(s)], float(s)) for s in range(N)][-1]
 
-    arr1 = [("a1", 14), oc, osc]
+    arr1 = [("a1", loc1), oc, osc]
     L1 = (T.land1[:], T.land1s[:])
     t = MM(arr1 + free1, T.pss[:, 0:128], L1, U)
     tB2 = MM([], T.psb[:, 0:128], U, L1)
-    V([tB2, c_k3], "ts", T.g2[:, 0:128], T.psb[:, 0:128], T.pss[:, 0:1], -1.0, A.is_equal, A.mult)
+    V([tB2], "ts", T.g2[:, 0:128], T.psb[:, 0:128], T.pss[:, 0:1], -1.0, A.is_equal, A.mult)
     e2 = V([], "ts", T.g2[:, 128:256], T.psb[:, 0:128], T.pss[:, 0:1], None, A.is_ge)
     r2 = V([e2], "scan", T.r2[:], T.mk2[:], T.g2[:], 0.0, A.mult, A.add)
     t = V([r2], "copy", T.r2f[:], T.r2[:, 255:256])
@@ -260,43 +292,44 @@ def rank_program(g, core, T, topo):
     t = V([t, c_seg], "scan", T.s2[:], T.seg[:], T.ot2[:], 0.0, A.mult, A.add)
     off2 = fold([t], lambda a: T.s2[a:a + 64, 31:192:32], T.t2, T.u2, T.kb, 0.0)[1]
     me2 = c128(rank, K2)
-    pc = V(off2 + arr1, "copy", u32(T.snd2[:]), u32(T.land1[:]).indirect(T.kb[:, 0:2]))
-    psc = ACT(off2 + arr1, T.snd2s[:], T.land1s[:].indirect(T.kb[:, 0:2]), F.Copy)
+    pc = V(off2 + arr1, "copy", u32(T.snd2[:, 0:32]), u32(T.land1[:]).indirect(T.kb[:, 0:2]))
+    psc = ACT(off2 + arr1, T.snd2s[:, 0:32], T.land1s[:].indirect(T.kb[:, 0:2]), F.Copy)
+    ok = V([], "copy", T.kl[:, rank, 0:4], T.kb[:, 2:6])
     need("pool", off2)
     loc += fused(g, T, topo, "ak", off[1:], [(d, T.kb[:, 2:6], T.kl[:, rank, 0:4]) for d in ring])
-    ok = V([], "copy", T.kl[:, rank, 0:4], T.kb[:, 2:6])
     need("pool", [psc])
-    loc += fused(g, T, topo, "hx", on, [(h[0], T.snd2s[:, 0:K2], T.hps[:]) for h in hs if h[1] == "planes"])
+    loc += fused(g, T, topo, "hx", on, [(h[0], T.snd2s[:, 0:K2], T.hps[:]) for h in hs[0:2]])
     need("pool", [pc])
-    loc += fused(g, T, topo, "a2", off[:-1], [(d, u8(T.snd2[:, 0:K2]), u8(T.land2[:, me2])) for d in ring])
-    dc = dma("sync", [pc], u8(T.land2[:, me2]), u8(T.snd2[:, 0:K2]), "dc")
+    loc += fused(g, T, topo, "hx", on, [(hs[2][0], u8(T.snd2[:, 0:K2]), u8(T.hq[:]))])
+    loc += fused(g, T, topo, "a2", off, [(T.cores[d], u8(T.snd2[:, 0:K2]), u8(T.land2[:, me2])) for d in hs[0][2]])
     at = ("at", sum(len(off) // len(h[3]) for r in range(N) for h in helpers(r, T, topo) if rank in h[3]))
     dt1 = dma("sync", [at, dt0, c_tab], T.tab[1:2, :], T.tabd[:], "dt1")
 
     ak = ("ak", N - 1)
-    kf = V([ak, ok], "copy", T.kf[:], T.kl[:, :, 2:4])
+    kf = V([ak, ok, c_k3], "copy", T.kf[:], T.kl[:, :, 2:4])
     xr = [ACT([kf], T.xr[:, c128(b, 32)], T.z32[:], F.Identity, bias=T.kf[:, 2 * b:2 * b + 1]) for b in range(8)]
     t = [V([kf], "tt", T.mk[:, 9 * c:9 * c + 8], T.kf[:, 1:16:2], T.m1[:, c128(c, 8)], A.mult) for c in range(2)]
     kp = [V([t[c]], "red", T.kp[:, c:c + 1], T.mk[:, c128(c, 9)], AxisListType.X, A.add) for c in range(2)]
     koff = [V([], "copy", T.koff[:], T.kl[:, :, 0:2])]
     idr = V(xr, "tr", T.idr[:], T.xr[:])
+    num = V(koff + [dt1], "copy", T.num[:], T.tab[:].indirect(T.koff[:]))
     lanes = (slice(0, 128), slice(96, 128))
     tie = [ACT([idr] + kp, T.tie[lanes[c], c128(c, M)], T.idr[lanes[c], :, 0:K2], F.Relu, bias=T.kp[lanes[c], c:c + 1], scale=KS) for c in range(2)]
 
-    arr2 = [("a2", N - 1 + 2 * N), dc]
+    arr2 = [("a2", 4 * N)]
     L2 = (T.land2[:], T.land2s[:])
-    tS3 = [MM(arr2 + [e2] + free1, T.pss[:, 512 * c + 512:512 * c + 640], (T.land2[:, 32 * c:32 * c + 128], T.land2s[:, 32 * c:32 * c + 128]), U) for c in range(2)]
+    tS3 = [MM(arr2 + [e2] + free1, T.pss[:, 512:640], (T.land2[:, 0:128], T.land2s[:, 0:128]), U)]
     tB3 = MM([], T.psb[:, 512:512 + M], U, L2)
+    tS3.append(MM([], T.pss[:, 1024:1152], (T.land2[:, 32:M], T.land2s[:, 32:M]), U))
     yps = [T.psb[:, 1024:1024 + M], T.psb[:, 1536:1536 + M], T.pss[:, 1536:1536 + M]]
     tY = [MM([wq], yps[o], (T.wq[:, c128(o)], T.ws[:, c128(o)]), L2) for o in range(3)]
-    sc3 = ACT(tS3, T.sc3[:], T.pss[:, 512:1025:512], F.Copy)
-    st3 = [ACT([sc3, tie[c]], T.st3[lanes[c], c128(c, M)], T.tie[lanes[c], c128(c, M)], F.Identity, bias=T.sc3[lanes[c], c:c + 1]) for c in range(2)]
+    sc3 = [ACT([tS3[c]], T.sc3[:, c:c + 1], T.pss[:, 512 * c + 512:512 * c + 513], F.Copy) for c in range(2)]
+    st3 = [ACT([sc3[c], tie[c]], T.st3[lanes[c], c128(c, M)], T.tie[lanes[c], c128(c, M)], F.Identity, bias=T.sc3[lanes[c], c:c + 1]) for c in range(2)]
     ysb = [ACT([tY[o]], T.ysb[:, c128(o, M)], yps[o], F.Copy) for o in range(3)]
-    t = ACT(koff + [dt1], T.num[:], T.tab[:].indirect(T.koff[:]), F.Copy)
-    nump = ACT([t, c_pk], T.nump[:], T.num[:].indirect(T.pk[:]), F.Copy)
+    nump = ACT([num, c_pk], T.nump[:], T.num[:].indirect(T.pk[:]), F.Copy)
     g3, e3, r3, oh3 = {}, {}, {}, {}
     for c in range(2):
-        g3[c] = V([tB3, sc3], "ts", T.g3[lanes[c], c128(2 * c, M)], T.psb[lanes[c], 512:512 + M], T.sc3[lanes[c], c:c + 1], None, A.is_gt)
+        g3[c] = V([tB3, sc3[c]], "ts", T.g3[lanes[c], c128(2 * c, M)], T.psb[lanes[c], 512:512 + M], T.sc3[lanes[c], c:c + 1], None, A.is_gt)
     for c in range(2):
         e3[c] = V([st3[c]], "tt", T.g3[lanes[c], c128(2 * c + 1, M)], T.psb[lanes[c], 512:512 + M], T.st3[lanes[c], c128(c, M)], A.is_equal)
     for c in range(2):
@@ -310,7 +343,7 @@ def rank_program(g, core, T, topo):
     y0 = V(off3 + ysb, "copy", T.yo[:, c128(0)], T.ysb[:, c128(0, M)].indirect(T.off3[:]))
     y1 = ACT(off3 + ysb, T.yo[:, c128(1)], T.ysb[:, c128(1, M)].indirect(T.off3[:]), F.Copy)
     y2 = V([], "copy", T.yo[:, c128(2)], T.ysb[:, c128(2, M)].indirect(T.off3[:]))
-    ido = ACT([nump], T.ido[:], T.nump[:].indirect(T.off3[:]), F.Identity, bias=T.b256[:])
+    ido = ACT([nump, c_k3], T.ido[:], T.nump[:].indirect(T.off3[:]), F.Identity, bias=T.b256[:])
     outs = [dma("sync", [y0, y1], T.y[:, 0:256], T.yo[:, 0:256], "dy0"), dma("sync", [y2], T.y[:, c128(2)], T.yo[:, c128(2)], "dy1"),
             dma("sca", [ido], T["id"][:], T.ido[0:2, :], "di")]
     need("pool", list(cnt.items()) + arr1 + arr2 + [ak, at, dt1, ("loc", loc), du, dw] + dx + outs)

@@ -8,17 +8,19 @@ SCRATCH = {"psb": ("psum", [128, 2048], "float32"), "pss": ("psum", [128, 2048],
            "tabd": ("dram", [N, 128, 1], "float32"), "thop": ("dram", [128, 1], "float32")}
 for _d, _l in (("float8_e4m3fn_x4", "xq 512 uq 128 ur 128 wq 384 snd1 128 land1 128 snd2 32 hq 20 land2 160"),
                ("uint8", "xs 512 us 128 urs 128 ws 384 snd1s 128 land1s 128 snd2s 32 hps 20 land2s 160"),
-               ("bfloat16", "xb 2048 ub 512 wb 1536 k2 192 k3 256 jb 4 j3 2 pf 1 g1 2048 r1 1024 on2 256 mk2 256 g2 256 r2 256"
-                " g3 640 r3 320 oh3 512 ot3 512"),
-               ("float16", "oh2 192 ot2 192 seg 192 s2 192 sm3 257"),
+               ("bfloat16", "xb 2048 ub 512 wb 1536 k2 192 k3 256 jb 4 j3 2 g1 2048 r1 1024 on2 256 mk2 256 g2 256"
+                " g3 640 r3 320 oh3 512"),
+               ("float16", "oh2 192"),
                ("uint16", "zoff 8 off1 8 kb 6 koff 16 off3 8 pk 10"), ("int32", "pi 1 si 1 bi 1 ci 1 jq 10"),
-               ("float32", "z32 32 zt 128 tri 128 ms 16 m0 16 m1 16 mk 18 sc1 4 st1 512 up1 4 ge1 4 u1 8 r2f 1 p8 1 key 1 t2 6 u2 6"
-                " kf 16 xr 256 kp 2 tie 320 sc3 2 st3 320 d3 8 t3 8 u3 8 ysb 480 yo 384 tab 1024 num 256 pm 1 j16 10 jj 10 jr 10 nump 160 b256 1 ido 128")):
+               ("float32", "z32 32 zt 128 tri 128 ms 16 m0 16 m1 16 mk 18 sc1 4 st1 512 up1 4 ge1 4 u1 8 r2 256 pf 1 p8 1 key 1"
+                " kf 16 xr 256 kp 2 tie 320 sc3 1 st3 320 ysb 480 yo 384 tab 1024 num 256 pm 1 j16 10 jj 10 jr 10 nump 160 b256 1 ido 128")):
     _w = _l.split()
     for _i in range(0, len(_w), 2):
         SCRATCH[_w[_i]] = ("sbuf", [128, int(_w[_i + 1])], _d)
-for _n, _k in (("krow1", 32), ("krow2", 32), ("krow3", 32), ("oh1", 128), ("ot1", 128), ("sm1", 128)):
+for _n, _k in (("krow1", 32), ("krow2", 32), ("krow3", 32), ("oh1", 128), ("ot1", 128), ("sm1", 128), ("ot3", 96), ("sm3", 96)):
     SCRATCH[_n] = ("sbuf", [128, 8, _k], "bfloat16")
+for _n in ("ot2", "s2"):
+    SCRATCH[_n] = ("sbuf", [128, 6, 64], "float16")
 for _n in ("sg", "sh"):
     SCRATCH[_n] = ("sbuf", [128, 2, 384], "bfloat16")
 SCRATCH["idr"] = ("sbuf", [128, 8, 32], "float32")
@@ -128,13 +130,9 @@ def rank_program(g, core, T, topo):
     def c128(i, w=128):
         return slice(w * i, w * i + w)
 
-    def fold(toks, src, t, u, *last):
-        if t is None:
-            b = [V(toks, "tt", u[p:p + 32, :], src(0), src(32), A.add) for p in (0, 32)]
-        else:
-            a = V(toks, "tt", t[0:64, :], src(0), src(64), A.add)
-            b = [V([a], "tt", u[p:p + 32, :], t[0:32, :], t[32:64, :], A.add) for p in (0, 32)]
-        return b, [V(b, "ts", last[0][p:p + 64, :], u[0:64, :], last[1], None, A.add) for p in (0, 64)]
+    def lists(toks, ot, sm, n, out):
+        t = [V(toks, "scan", sm[0:32, b, :], ot[0:32, b, :], ot[32:64, b, :], 0.0, A.add, A.add) for b in range(n)]
+        return [V(t, "copy", out[p:p + 32, :], sm[0:32, :, sm.shape[2] - 1]) for p in (0, 32, 64, 96)]
 
     du = dma("sca", [], T.ub[:, 0:8], T.u[:, 0:8], "du")
     dx = [dma("sync", [], T.xb[:, c128(i, 512)], T.x[:, c128(i, 512)], "dx%d" % i) for i in range(4)]
@@ -147,10 +145,7 @@ def rank_program(g, core, T, topo):
     c_on = V([], "set", T.on2[:], 1.0)
     V([], "set", T.z32[:], 0.0)
     V([], "set", T.mk[:, 8:18:9], 0.5 * KS)
-    V([], "set", T.oh3[:, 256:512], 0.0)
-    V([], "set", T.sm3[:, 0:1], 0.0)
-    t = V([], "set", T.seg[:], 1.0)
-    c_seg = V([t], "set", T.seg[:, 0:192:32], 0.0)
+    V([], "set", T.ot3[32:64, :, 64:96], 0.0)
     c_pi = done("pool", g.iota(T.pi[:], [[0, 1]], 0, 1))
     need("pool", [c_zt, c_on])
     c_tri = P(T.tri[:], T.zt[:], [[-1, 128]], A.is_gt, 1.0, 0, 1)
@@ -171,21 +166,22 @@ def rank_program(g, core, T, topo):
     c_k2 = IOTA(T.j16[:], [[16, M // 16]], 0, 1)
 
     t = V([du, c_ub], "qz", T.uq[:], T.us[:], T.ub[:])
-    c_ur = V([t, c_zoff], "copy", u32(T.ur[:]), u32(T.uq[:]).indirect(T.zoff[:]))
     c_us = ACT([t, c_zoff], T.urs[:], T.us[:].indirect(T.zoff[:]), F.Copy)
+    q0 = V([dx[0]], "qz", T.xq[:, 0:128], T.xs[:, 0:128], T.xb[:, 0:512])
+    c_ur = V([t, c_zoff], "copy", u32(T.ur[:]), u32(T.uq[:]).indirect(T.zoff[:]))
     U = (T.ur[:], T.urs[:])
 
     tq, tA, tB, sc, up, sg, ge, st, rk, oh, last = [{} for _ in range(11)]
 
     def quant(i):
         X = (T.xq[:, c128(i)], T.xs[:, c128(i)])
-        tq[i] = V([dx[i]], "qz", X[0], X[1], T.xb[:, c128(i, 512)])
-        t = MM([tq[i], c_ur, c_us], T.pss[:, 512 * i:512 * i + 128], X, U)
-        tB[i] = MM([], T.psb[:, 512 * i:512 * i + 128], U, X)
+        tq[i] = V([dx[i]], "qz", X[0], X[1], T.xb[:, c128(i, 512)]) if i else q0
+        t = MM([tq[i]], T.pss[:, 512 * i:512 * i + 128], X, (T.uq[:], T.us[:]))
+        tB[i] = MM([c_ur, c_us], T.psb[:, 512 * i:512 * i + 128], U, X)
         sc[i] = ACT([t], T.sc1[:, i:i + 1], T.pss[:, 512 * i:512 * i + 1], F.Copy)
         up[i] = ACT([], T.up1[:, i:i + 1], T.pss[:, 512 * i:512 * i + 1], F.Abs, bias=TINY, scale=STEP)
-        if i in (1, 2):
-            tA[i + 1] = MM([up[i - 1]], T.pss[:, 512 * i - 512:640 * i - 384], U, (T.xq[:, 0:128 * i + 128], T.xs[:, 0:128 * i + 128]))
+        if i >= 2:
+            tA[i] = MM([up[i - 2]], T.pss[:, 512 * i - 1024:640 * i - 1024], U, (T.xq[:, 0:128 * i], T.xs[:, 0:128 * i]))
         if i >= 2:
             sg[i] = ACT([tA[i], sc[i]], T.sg[:, i - 2, 0:128 * i], T.pss[:, 512 * i - 1024:640 * i - 1024], F.Sign, bias=T.sc1[:, i:i + 1], scale=-1.0)
         st[i] = ACT([up[i], c_tri], T.st1[:, c128(i)], T.tri[:], F.Identity, bias=T.sc1[:, i:i + 1], scale=T.up1[:, i:i + 1])
@@ -236,7 +232,8 @@ def rank_program(g, core, T, topo):
     turn(3)
     free1 = [last[3], sg[3]]
     sm = [V([tr[3]], "scan", T.sm1[0:64, b, :], T.ot1[0:64, b, :], T.ot1[64:128, b, :], 0.0, A.add, A.add) for b in range(8)]
-    l1, off1 = fold(sm, lambda a: T.sm1[a:a + 32, :, 127], None, T.u1, T.off1, 256.0)
+    l1 = [V(sm, "tt", T.u1[p:p + 32, :], T.sm1[0:32, :, 127], T.sm1[32:64, :, 127], A.add) for p in (0, 32)]
+    off1 = [V(l1, "ts", T.off1[p:p + 64, :], T.u1[0:64, :], 256.0, None, A.add) for p in (0, 64)]
     me1 = c128(rank, NB)
     pc = V(off1, "copy", u32(T.snd1[:]), u32(T.xq[:]).indirect(T.off1[:]))
     psc = ACT(off1, T.snd1s[:], T.xs[:].indirect(T.off1[:]), F.Copy)
@@ -285,12 +282,10 @@ def rank_program(g, core, T, topo):
     V([tB2], "ts", T.g2[:, 0:128], T.psb[:, 0:128], T.pss[:, 0:1], -1.0, A.is_equal, A.mult)
     e2 = V([], "ts", T.g2[:, 128:256], T.psb[:, 0:128], T.pss[:, 0:1], None, A.is_ge)
     r2 = V([e2], "scan", T.r2[:], T.mk2[:], T.g2[:], 0.0, A.mult, A.add)
-    t = V([r2], "copy", T.r2f[:], T.r2[:, 255:256])
-    V([], "ts", T.oh2[:, 0:64], T.k2[:, 0:64], T.r2[:, 255:256], T.pf[:], A.is_equal, A.mult)
-    t = V([t, c_key], "ts", T.oh2[:, 64:192], T.k2[:, 64:192], T.r2f[:], T.key[:], A.is_equal, A.mult)
-    t = V([t], "tr", T.ot2[:], T.oh2[:])
-    t = V([t, c_seg], "scan", T.s2[:], T.seg[:], T.ot2[:], 0.0, A.mult, A.add)
-    off2 = fold([t], lambda a: T.s2[a:a + 64, 31:192:32], T.t2, T.u2, T.kb, 0.0)[1]
+    V([r2], "ts", T.oh2[:, 0:64], T.k2[:, 0:64], T.r2[:, 255:256], T.pf[:], A.is_equal, A.mult)
+    t = V([c_key], "ts", T.oh2[:, 64:192], T.k2[:, 64:192], T.r2[:, 255:256], T.key[:], A.is_equal, A.mult)
+    t = [V([t], "tr", T.ot2[0:64, :, c128(a, 32)], T.oh2[c128(a, 64), :]) for a in range(2)]
+    off2 = lists(t, T.ot2, T.s2, 6, T.kb)
     me2 = c128(rank, K2)
     pc = V(off2 + arr1, "copy", u32(T.snd2[:, 0:32]), u32(T.land1[:]).indirect(T.kb[:, 0:2]))
     psc = ACT(off2 + arr1, T.snd2s[:, 0:32], T.land1s[:].indirect(T.kb[:, 0:2]), F.Copy)
@@ -320,26 +315,27 @@ def rank_program(g, core, T, topo):
     L2 = (T.land2[:], T.land2s[:])
     tS3 = [MM(arr2 + [e2] + free1, T.pss[:, 512:640], (T.land2[:, 0:128], T.land2s[:, 0:128]), U)]
     tB3 = MM([], T.psb[:, 512:512 + M], U, L2)
+    tA3 = MM([], T.psb[:, 0:128], (T.land2[:, 32:M], T.land2s[:, 32:M]), U)
     tS3.append(MM([], T.pss[:, 1024:1152], (T.land2[:, 32:M], T.land2s[:, 32:M]), U))
     yps = [T.psb[:, 1024:1024 + M], T.psb[:, 1536:1536 + M], T.pss[:, 1536:1536 + M]]
     tY = [MM([wq], yps[o], (T.wq[:, c128(o)], T.ws[:, c128(o)]), L2) for o in range(3)]
-    sc3 = [ACT([tS3[c]], T.sc3[:, c:c + 1], T.pss[:, 512 * c + 512:512 * c + 513], F.Copy) for c in range(2)]
-    st3 = [ACT([sc3[c], tie[c]], T.st3[lanes[c], c128(c, M)], T.tie[lanes[c], c128(c, M)], F.Identity, bias=T.sc3[lanes[c], c:c + 1]) for c in range(2)]
+    sc1 = ACT([tA3], T.sc3[:], T.psb[:, 0:1], F.Copy)
+    st3 = {1: ACT([sc1, tie[1]], T.st3[lanes[1], c128(1, M)], T.tie[lanes[1], c128(1, M)], F.Identity, bias=T.sc3[lanes[1], :])}
     ysb = [ACT([tY[o]], T.ysb[:, c128(o, M)], yps[o], F.Copy) for o in range(3)]
     nump = ACT([num, c_pk], T.nump[:], T.num[:].indirect(T.pk[:]), F.Copy)
     g3, e3, r3, oh3 = {}, {}, {}, {}
+    st3[0] = V([tS3[0], tie[0]], "ts", T.st3[:, 0:M], T.tie[:, 0:M], T.pss[:, 512:513], None, A.add)
     for c in range(2):
-        g3[c] = V([tB3, sc3[c]], "ts", T.g3[lanes[c], c128(2 * c, M)], T.psb[lanes[c], 512:512 + M], T.sc3[lanes[c], c:c + 1], None, A.is_gt)
+        g3[c] = V([tB3, tS3[c]], "ts", T.g3[lanes[c], c128(2 * c, M)], T.psb[lanes[c], 512:512 + M], T.pss[lanes[c], 512 * c + 512:512 * c + 513], None, A.is_gt)
     for c in range(2):
         e3[c] = V([st3[c]], "tt", T.g3[lanes[c], c128(2 * c + 1, M)], T.psb[lanes[c], 512:512 + M], T.st3[lanes[c], c128(c, M)], A.is_equal)
     for c in range(2):
         r3[c] = V([g3[c], e3[c]], "scan", T.r3[lanes[c], c128(c, M)], T.g3[lanes[c], c128(2 * c, M)], T.g3[lanes[c], c128(2 * c + 1, M)], 0.0, A.add, A.add)
     for c in range(2):
         oh3[c] = V([r3[c]], "ts", T.oh3[lanes[c], c128(c, 256)], T.k3[lanes[c], :], T.r3[lanes[c], M * c + M - 1:M * c + M], T.j3[lanes[c], c:c + 1], A.is_equal, A.mult)
-    t = V(list(oh3.values()), "tr", T.ot3[:], T.oh3[:])
-    t = V([t], "scan", T.sm3[:, 1:257], T.ot3[:, 0:256], T.ot3[:, 256:512], 0.0, A.add, A.add)
-    t = V([t], "tt", T.d3[:], T.sm3[:, 32:257:32], T.sm3[:, 0:256:32], A.subtract)
-    off3 = fold([t], lambda a: T.d3[a:a + 64, :], T.t3, T.u3, T.off3, 0.0)[1]
+    t = [V([oh3[0]], "tr", T.ot3[0:64, :, 0:32], T.oh3[0:64, 0:256]), V([], "tr", T.ot3[0:64, :, 32:64], T.oh3[64:128, 0:256]),
+         V([oh3[1]], "tr", T.ot3[0:32, :, 64:96], T.oh3[96:128, 256:512])]
+    off3 = lists(t, T.ot3, T.sm3, 8, T.off3)
     y0 = V(off3 + ysb, "copy", T.yo[:, c128(0)], T.ysb[:, c128(0, M)].indirect(T.off3[:]))
     y1 = ACT(off3 + ysb, T.yo[:, c128(1)], T.ysb[:, c128(1, M)].indirect(T.off3[:]), F.Copy)
     y2 = V([], "copy", T.yo[:, c128(2)], T.ysb[:, c128(2, M)].indirect(T.off3[:]))

@@ -5,26 +5,24 @@ N, NB, K2, KS = 8, 16, 20, 2.0 ** 80
 STEP, TINY = 0.625 * 2.0 ** -23, 2.0 ** -124
 M = N * K2
 SCRATCH = {"psb": ("psum", [128, 2048], "float32"), "pss": ("psum", [128, 2048], "float32"),
-           "tabd": ("dram", [N, 128, 1], "float32"), "thop": ("dram", [128, 1], "float32")}
+           "tabd": ("dram", [N, 128, 1], "bfloat16"), "thop": ("dram", [128, 1], "bfloat16")}
 for _d, _l in (("float8_e4m3fn_x4", "xq 512 uq 128 ur 128 wq 384 snd1 128 land1 128 snd2 32 hq 20 land2 160"),
                ("uint8", "xs 512 us 128 urs 128 ws 384 snd1s 128 land1s 128 snd2s 32 hps 20 land2s 160"),
                ("bfloat16", "xb 2048 ub 512 wb 1536 k2 192 k3 256 jb 4 j3 2 g1 2048 r1 1024 on2 256 mk2 256 g2 256"
-                " g3 640 r3 320 oh3 512"),
+                " g3 640 r3 320 oh3 512 u1 8 tab 1024 sg 384 sh 384"),
                ("float16", "oh2 192"),
-               ("uint16", "zoff 8 off1 8 kb 6 koff 16 off3 8 pk 10"), ("int32", "pi 1 si 1 bi 1 ci 1 jq 10"),
-               ("float32", "z32 32 zt 128 tri 128 ms 16 m0 16 m1 16 mk 18 sc1 4 st1 512 up1 4 ge1 4 u1 8 r2 256 pf 1 p8 1 key 1"
-                " kf 16 xr 256 kp 2 tie 320 sc3 1 st3 320 ysb 480 yo 384 tab 1024 num 256 pm 1 j16 10 jj 10 jr 10 nump 160 b256 1 ido 128")):
+               ("uint16", "zoff 8 off1 8 kb 2 koff 16 off3 8 pk 10"), ("int32", "pi 1 si 1 bi 1 ci 1 jq 10"),
+               ("float32", "z32 32 zt 128 tri 128 ms 16 m0 16 m1 16 mk 18 sc1 4 st1 512 up1 4 ge1 1 r2 256 pf 1 p8 1 key 1"
+                " xr 256 kp 2 st3 320 ysb 480 yo 384 hk 4 num 256 pm 1 j16 10 jj 10 jr 10 nump 160 b256 1 ido 128")):
     _w = _l.split()
     for _i in range(0, len(_w), 2):
         SCRATCH[_w[_i]] = ("sbuf", [128, int(_w[_i + 1])], _d)
-for _n, _k in (("krow1", 32), ("krow2", 32), ("krow3", 32), ("oh1", 128), ("ot1", 128), ("sm1", 128), ("ot3", 96), ("sm3", 96)):
+for _n, _k in (("krow", 32), ("krow3", 32), ("oh1", 128), ("ot1", 128), ("sm1", 128), ("ot3", 96), ("sm3", 96)):
     SCRATCH[_n] = ("sbuf", [128, 8, _k], "bfloat16")
-for _n in ("ot2", "s2"):
-    SCRATCH[_n] = ("sbuf", [128, 6, 64], "float16")
-for _n in ("sg", "sh"):
-    SCRATCH[_n] = ("sbuf", [128, 2, 384], "bfloat16")
+SCRATCH["ot2"] = ("sbuf", [128, 6, 64], "float16")
+SCRATCH["s2"] = ("sbuf", [128, 6, 64], "float32")
 SCRATCH["idr"] = ("sbuf", [128, 8, 32], "float32")
-SCRATCH["kl"] = ("sbuf", [128, 8, 8], "uint16")
+SCRATCH["kl"] = ("sbuf", [128, 8, 4], "float32")
 SEMAPHORES = "vec sca ten pool du dx0 dx1 dx2 dx3 dw a1 a2 ak at ht hx loc dt0 dt1 dy0 dy1 di".split()
 
 
@@ -36,7 +34,8 @@ def helpers(r, T, topo):
     ring = [(r + b) % N for b in range(1, N + 1)]
     near = [d for d in ring if topo.may_write(plain[0], T.cores[d])]
     far = [d for d in ring if d not in near]
-    return [(wide[0], "planes", far, far), (plain[0], "planes", near, near[:2]), (plain[1], "codes", near, near[2:-1])]
+    return [(wide[0], "keys", far, far), (plain[2], "keys", near[:-1], near[0:1]),
+            (plain[0], "codes", near, near[1:2]), (plain[1], "planes", near, near[2:3])]
 
 
 def fused(g, T, topo, sem, engines, jobs, share=None):
@@ -61,12 +60,10 @@ def hand_on(g, core, r, what, to, tab_to, T, topo):
     off, on = engines_of(core, T, topo)
     g.wait_ge(T.sem.ht, len(on) // 4)
     n = fused(g, T, topo, "at", off, [(T.cores[d], T.thop[:], T.tabd[r]) for d in tab_to])
-    g.wait_ge(T.sem.hx, len(on) // (2 if what == "planes" else 1))
-    if what == "planes":
-        src, dst = T.hps[:, 0:K2], T.land2s[:, K2 * r:K2 * r + K2]
-    else:
-        src, dst = T.hq[:].bitcast(dt.uint8), T.land2[:, K2 * r:K2 * r + K2].bitcast(dt.uint8)
-    n += fused(g, T, topo, "a2", off, [(T.cores[d], src, dst) for d in to])
+    g.wait_ge(T.sem.hx, len(on))
+    src, dst = {"planes": (T.hps[:], T.land2s[:, K2 * r:K2 * r + K2]), "keys": (T.hk[:], T.kl[:, r, :]),
+                "codes": (T.hq[:].bitcast(dt.uint8), T.land2[:, K2 * r:K2 * r + K2].bitcast(dt.uint8))}[what]
+    n += fused(g, T, topo, "ak" if what == "keys" else "a2", off, [(T.cores[d], src, dst) for d in to])
     g.wait_ge(T.sem.loc, n)
 
 
@@ -130,9 +127,8 @@ def rank_program(g, core, T, topo):
     def c128(i, w=128):
         return slice(w * i, w * i + w)
 
-    def lists(toks, ot, sm, n, out):
-        t = [V(toks, "scan", sm[0:32, b, :], ot[0:32, b, :], ot[32:64, b, :], 0.0, A.add, A.add) for b in range(n)]
-        return [V(t, "copy", out[p:p + 32, :], sm[0:32, :, sm.shape[2] - 1]) for p in (0, 32, 64, 96)]
+    def sums(toks, ot, sm, blocks):
+        return [V(toks, "scan", sm[0:32, b, :], ot[0:32, b, :], ot[32:64, b, :], 0.0, A.add, A.add) for b in blocks]
 
     du = dma("sca", [], T.ub[:, 0:8], T.u[:, 0:8], "du")
     dx = [dma("sync", [], T.xb[:, c128(i, 512)], T.x[:, c128(i, 512)], "dx%d" % i) for i in range(4)]
@@ -141,7 +137,7 @@ def rank_program(g, core, T, topo):
     c_ub = V([], "set", T.ub[:, 8:512], 0.0)
     c_zoff = V([], "set", T.zoff[:], 0)
     c_zt = V([], "set", T.zt[:], 0.0)
-    V([], "set", T.ms[:], -KS)
+    V([], "set", T.ms[:], -1.0)
     c_on = V([], "set", T.on2[:], 1.0)
     V([], "set", T.z32[:], 0.0)
     V([], "set", T.mk[:, 8:18:9], 0.5 * KS)
@@ -150,8 +146,7 @@ def rank_program(g, core, T, topo):
     need("pool", [c_zt, c_on])
     c_tri = P(T.tri[:], T.zt[:], [[-1, 128]], A.is_gt, 1.0, 0, 1)
     IOTA(T.jb[:], [[128, 4]], -256, 1)
-    IOTA(T.krow1[:], [[1, 8], [0, 2], [8, 16]], 0, 0)
-    IOTA(T.krow2[:], [[2, 8], [0, 2], [16, 16]], -256, 0)
+    IOTA(T.krow[:], [[1, 8], [0, 2], [8, 16]], 0, 0)
     c_kr = IOTA(T.krow3[:], [[2, 8], [0, 2], [16, 16]], -384, 0)
     P(T.mk2[:], T.on2[:], [[-1, 256]], A.not_equal, 0.0, 0, 1)
     IOTA(T.pf[:], [[0, 1]], 0, 1)
@@ -165,28 +160,24 @@ def rank_program(g, core, T, topo):
         IOTA(T.k2[:, a:a + 64], [[16, 2], [0, 2], [1, 16]], 0, 0)
     c_k2 = IOTA(T.j16[:], [[16, M // 16]], 0, 1)
 
-    t = V([du, c_ub], "qz", T.uq[:], T.us[:], T.ub[:])
-    c_us = ACT([t, c_zoff], T.urs[:], T.us[:].indirect(T.zoff[:]), F.Copy)
-    q0 = V([dx[0]], "qz", T.xq[:, 0:128], T.xs[:, 0:128], T.xb[:, 0:512])
-    c_ur = V([t, c_zoff], "copy", u32(T.ur[:]), u32(T.uq[:]).indirect(T.zoff[:]))
+    qu = V([du, c_ub], "qz", T.uq[:], T.us[:], T.ub[:])
+    c_us = ACT([qu, c_zoff], T.urs[:], T.us[:].indirect(T.zoff[:]), F.Copy)
     U = (T.ur[:], T.urs[:])
 
-    tq, tA, tB, sc, up, sg, ge, st, rk, oh, last = [{} for _ in range(11)]
+    tq, tS, tB, sc, up, st, rk, oh, tr, last = [{} for _ in range(10)]
 
     def quant(i):
-        X = (T.xq[:, c128(i)], T.xs[:, c128(i)])
-        tq[i] = V([dx[i]], "qz", X[0], X[1], T.xb[:, c128(i, 512)]) if i else q0
-        t = MM([tq[i]], T.pss[:, 512 * i:512 * i + 128], X, (T.uq[:], T.us[:]))
-        tB[i] = MM([c_ur, c_us], T.psb[:, 512 * i:512 * i + 128], U, X)
-        sc[i] = ACT([t], T.sc1[:, i:i + 1], T.pss[:, 512 * i:512 * i + 1], F.Copy)
+        tq[i] = V([dx[i]], "qz", T.xq[:, c128(i)], T.xs[:, c128(i)], T.xb[:, c128(i, 512)])
+
+    def lane(i):
+        tS[i] = MM([tq[i]], T.pss[:, 512 * i:512 * i + 128], (T.xq[:, c128(i)], T.xs[:, c128(i)]), (T.uq[:], T.us[:]))
+
+    def score(i):
+        sc[i] = ACT([tS[i]], T.sc1[:, i:i + 1], T.pss[:, 512 * i:512 * i + 1], F.Copy)
         up[i] = ACT([], T.up1[:, i:i + 1], T.pss[:, 512 * i:512 * i + 1], F.Abs, bias=TINY, scale=STEP)
-        if i >= 2:
-            tA[i] = MM([up[i - 2]], T.pss[:, 512 * i - 1024:640 * i - 1024], U, (T.xq[:, 0:128 * i], T.xs[:, 0:128 * i]))
-        if i >= 2:
-            sg[i] = ACT([tA[i], sc[i]], T.sg[:, i - 2, 0:128 * i], T.pss[:, 512 * i - 1024:640 * i - 1024], F.Sign, bias=T.sc1[:, i:i + 1], scale=-1.0)
+
+    def level(i):
         st[i] = ACT([up[i], c_tri], T.st1[:, c128(i)], T.tri[:], F.Identity, bias=T.sc1[:, i:i + 1], scale=T.up1[:, i:i + 1])
-        if i >= 2:
-            ge[i] = ACT([sg[i]], T.sh[:, i - 2, 0:128 * i], T.sg[:, i - 2, 0:128 * i], F.Sign, bias=0.5, scale=-1.0, accum_out=T.ge1[:, i:i + 1])
 
     def blocks(*ci):
         for c, i in ci:
@@ -197,40 +188,50 @@ def rank_program(g, core, T, topo):
                 last[c] = V([tB[i], sc[c]], "ts", out, s, T.sc1[:, c:c + 1], None, A.is_ge if i < c else A.is_gt)
 
     def count(c):
-        if c < 2:
+        if c < 3:
             rk[c] = V([last[c]], "scan", T.r1[:, c128(c, 256)], T.g1[:, 512 * c:512 * c + 256], T.g1[:, 512 * c + 256:512 * c + 512], 0.0, A.add, A.add)
         else:
-            own = T.g1[:, 640 * c:512 * c + 512]
-            rk[c] = V([last[c], ge[c]], "scan", T.r1[:, 384 * c - 256:256 * c + 256], own, own, T.ge1[:, c:c + 1], A.add, A.add)
+            rk[c] = V([last[c], ge], "scan", T.r1[:, 896:1024], T.g1[:, 1920:2048], T.g1[:, 1920:2048], T.ge1[:], A.add, A.add)
 
     def onehot(c):
-        oh[c] = V([rk[c], c_kr], "ts", T.oh1[:, :, c128(c, 32)], T["krow%d" % max(c, 1)][:], T.r1[:, 256 * c + 255:256 * c + 256], T.jb[:, c:c + 1], A.is_equal, A.mult)
+        oh[c] = V([rk[c], c_kr], "ts", T.oh1[:, :, c128(c, 32)], (T.krow3 if c == 3 else T.krow)[:], T.r1[:, 256 * c + 255:256 * c + 256], T.jb[:, c:c + 1], A.is_equal, A.mult)
 
     def turn(c):
         tr[c] = V([oh[c]], "tr", T.ot1[:, :, c128(c, 32)], T.oh1[:, :, c128(c, 32)])
 
-    tr = {}
     quant(0)
     quant(1)
+    c_ur = V([qu, c_zoff], "copy", u32(T.ur[:]), u32(T.uq[:]).indirect(T.zoff[:]))
     quant(2)
-    blocks((0, 1), (1, 0))
     quant(3)
-    blocks((0, 0), (0, 2), (1, 2), (1, 1), (0, 3), (1, 3))
+    for i in range(4):
+        if i != 1:
+            lane(i)
+        if i == 0:
+            lane(1)
+        tB[i] = MM([c_ur, c_us], T.psb[:, 512 * i:512 * i + 128], U, (T.xq[:, c128(i)], T.xs[:, c128(i)]))
+        score(i)
+        if i:
+            level(i - 1)
+    t = MM([up[0]], T.pss[:, 0:384], U, (T.xq[:, 0:384], T.xs[:, 0:384]))
+    sg = ACT([t, sc[3]], T.sg[:], T.pss[:, 0:384], F.Sign, bias=T.sc1[:, 3:4], scale=-1.0)
+    level(3)
+    ge = ACT([sg], T.sh[:], T.sg[:], F.Sign, bias=0.5, scale=-1.0, accum_out=T.ge1[:])
+    blocks((1, 0), (0, 1), (0, 0), (1, 2), (0, 2), (2, 0), (0, 3), (1, 1), (2, 1), (1, 3))
     count(0)
-    count(1)
     blocks((2, 3), (2, 2))
+    count(1)
     onehot(0)
-    onehot(1)
-    count(2)
-    turn(0)
     blocks((3, 3))
-    onehot(2)
-    turn(1)
+    count(2)
+    onehot(1)
     count(3)
-    turn(2)
+    turn(0)
+    onehot(2)
     onehot(3)
-    turn(3)
-    free1 = [last[3], sg[3]]
+    for c in (1, 2, 3):
+        turn(c)
+    free1 = [last[3], sg]
     sm = [V([tr[3]], "scan", T.sm1[0:64, b, :], T.ot1[0:64, b, :], T.ot1[64:128, b, :], 0.0, A.add, A.add) for b in range(8)]
     l1 = [V(sm, "tt", T.u1[p:p + 32, :], T.sm1[0:32, :, 127], T.sm1[32:64, :, 127], A.add) for p in (0, 32)]
     off1 = [V(l1, "ts", T.off1[p:p + 64, :], T.u1[0:64, :], 256.0, None, A.add) for p in (0, 64)]
@@ -282,60 +283,71 @@ def rank_program(g, core, T, topo):
     V([tB2], "ts", T.g2[:, 0:128], T.psb[:, 0:128], T.pss[:, 0:1], -1.0, A.is_equal, A.mult)
     e2 = V([], "ts", T.g2[:, 128:256], T.psb[:, 0:128], T.pss[:, 0:1], None, A.is_ge)
     r2 = V([e2], "scan", T.r2[:], T.mk2[:], T.g2[:], 0.0, A.mult, A.add)
-    V([r2], "ts", T.oh2[:, 0:64], T.k2[:, 0:64], T.r2[:, 255:256], T.pf[:], A.is_equal, A.mult)
-    t = V([c_key], "ts", T.oh2[:, 64:192], T.k2[:, 64:192], T.r2[:, 255:256], T.key[:], A.is_equal, A.mult)
-    t = [V([t], "tr", T.ot2[0:64, :, c128(a, 32)], T.oh2[c128(a, 64), :]) for a in range(2)]
-    off2 = lists(t, T.ot2, T.s2, 6, T.kb)
+    tk = V([r2, c_key], "ts", T.oh2[:, 64:192], T.k2[:, 64:192], T.r2[:, 255:256], T.key[:], A.is_equal, A.mult)
+    tp = V([], "ts", T.oh2[:, 0:64], T.k2[:, 0:64], T.r2[:, 255:256], T.pf[:], A.is_equal, A.mult)
+    tk = [V([tk], "tr", T.ot2[0:64, 2:6, c128(a, 32)], T.oh2[c128(a, 64), 64:192]) for a in range(2)]
+    tp = [V([tp], "tr", T.ot2[0:64, 0:2, c128(a, 32)], T.oh2[c128(a, 64), 0:64]) for a in range(2)]
+    tk = sums(tk, T.ot2, T.s2, range(2, 6))
+    tp = sums(tp, T.ot2, T.s2, range(2))
+    ks = [V(tp, "ts", T.kl[p:p + 32, rank, :], T.s2[0:32, 2:6, 63], KS, None, A.mult) for p in (0, 32)]
+    ks += [ACT(tk, T.kl[p:p + 32, rank, :], T.s2[0:32, 2:6, 63], F.Identity, scale=KS) for p in (64, 96)]
+    off2 = [V(tp, "copy", T.kb[p:p + 32, :], T.s2[0:32, 0:2, 63]) for p in (0, 32, 64, 96)]
     me2 = c128(rank, K2)
     pc = V(off2 + arr1, "copy", u32(T.snd2[:, 0:32]), u32(T.land1[:]).indirect(T.kb[:, 0:2]))
     psc = ACT(off2 + arr1, T.snd2s[:, 0:32], T.land1s[:].indirect(T.kb[:, 0:2]), F.Copy)
-    ok = V([], "copy", T.kl[:, rank, 0:4], T.kb[:, 2:6])
-    need("pool", off2)
-    loc += fused(g, T, topo, "ak", off[1:], [(d, T.kb[:, 2:6], T.kl[:, rank, 0:4]) for d in ring])
-    need("pool", [psc])
-    loc += fused(g, T, topo, "hx", on, [(h[0], T.snd2s[:, 0:K2], T.hps[:]) for h in hs[0:2]])
+    need("pool", ks)
+    loc += fused(g, T, topo, "hx", off + on, [(h[0], T.kl[:, rank, :], T.hk[:]) for h in hs[0:2]])
+    far = [T.cores[d] for d in hs[0][2]]
     need("pool", [pc])
     loc += fused(g, T, topo, "hx", on, [(hs[2][0], u8(T.snd2[:, 0:K2]), u8(T.hq[:]))])
-    loc += fused(g, T, topo, "a2", off, [(T.cores[d], u8(T.snd2[:, 0:K2]), u8(T.land2[:, me2])) for d in hs[0][2]])
+    loc += fused(g, T, topo, "a2", off, [(d, u8(T.snd2[:, 0:K2]), u8(T.land2[:, me2])) for d in far])
+    need("pool", [psc])
+    loc += fused(g, T, topo, "hx", on, [(hs[3][0], T.snd2s[:, 0:K2], T.hps[:])])
+    loc += fused(g, T, topo, "a2", off, [(d, T.snd2s[:, 0:K2], T.land2s[:, me2]) for d in far])
     at = ("at", sum(len(off) // len(h[3]) for r in range(N) for h in helpers(r, T, topo) if rank in h[3]))
     dt1 = dma("sync", [at, dt0, c_tab], T.tab[1:2, :], T.tabd[:], "dt1")
 
-    ak = ("ak", N - 1)
-    kf = V([ak, ok, c_k3], "copy", T.kf[:], T.kl[:, :, 2:4])
-    xr = [ACT([kf], T.xr[:, c128(b, 32)], T.z32[:], F.Identity, bias=T.kf[:, 2 * b:2 * b + 1]) for b in range(8)]
-    t = [V([kf], "tt", T.mk[:, 9 * c:9 * c + 8], T.kf[:, 1:16:2], T.m1[:, c128(c, 8)], A.mult) for c in range(2)]
-    kp = [V([t[c]], "red", T.kp[:, c:c + 1], T.mk[:, c128(c, 9)], AxisListType.X, A.add) for c in range(2)]
-    koff = [V([], "copy", T.koff[:], T.kl[:, :, 0:2])]
+    ak = ("ak", 2 * (N - 1))
+    xr = [ACT([ak] + ks, T.xr[:, c128(b, 32)], T.z32[:], F.Identity, bias=T.kl[:, b, 2:3]) for b in range(3)]
+    xr += [V([ak, c_k3] + ks, "ts", T.xr[:, c128(b, 32)], T.z32[:], T.kl[:, b, 2:3], None, A.add) for b in range(3, 8)]
+    t = [V([], "tt", T.mk[:, 9 * c:9 * c + 8], T.kl[:, :, 3], T.m1[:, c128(c, 8)], A.mult) for c in range(2)]
+    koff = V([], "ts", T.koff[:], T.kl[:, :, 0:2], 1.0 / KS, None, A.mult)
     idr = V(xr, "tr", T.idr[:], T.xr[:])
-    num = V(koff + [dt1], "copy", T.num[:], T.tab[:].indirect(T.koff[:]))
+    kp = [V([t[c]], "red", T.kp[:, c:c + 1], T.mk[:, c128(c, 9)], AxisListType.X, A.add) for c in range(2)]
+    num = ACT([koff, dt1], T.num[:], T.tab[:].indirect(T.koff[:]), F.Copy)
     lanes = (slice(0, 128), slice(96, 128))
-    tie = [ACT([idr] + kp, T.tie[lanes[c], c128(c, M)], T.idr[lanes[c], :, 0:K2], F.Relu, bias=T.kp[lanes[c], c:c + 1], scale=KS) for c in range(2)]
 
     arr2 = [("a2", 4 * N)]
     L2 = (T.land2[:], T.land2s[:])
     tS3 = [MM(arr2 + [e2] + free1, T.pss[:, 512:640], (T.land2[:, 0:128], T.land2s[:, 0:128]), U)]
     tB3 = MM([], T.psb[:, 512:512 + M], U, L2)
-    tA3 = MM([], T.psb[:, 0:128], (T.land2[:, 32:M], T.land2s[:, 32:M]), U)
     tS3.append(MM([], T.pss[:, 1024:1152], (T.land2[:, 32:M], T.land2s[:, 32:M]), U))
     yps = [T.psb[:, 1024:1024 + M], T.psb[:, 1536:1536 + M], T.pss[:, 1536:1536 + M]]
     tY = [MM([wq], yps[o], (T.wq[:, c128(o)], T.ws[:, c128(o)]), L2) for o in range(3)]
-    sc1 = ACT([tA3], T.sc3[:], T.psb[:, 0:1], F.Copy)
-    st3 = {1: ACT([sc1, tie[1]], T.st3[lanes[1], c128(1, M)], T.tie[lanes[1], c128(1, M)], F.Identity, bias=T.sc3[lanes[1], :])}
-    ysb = [ACT([tY[o]], T.ysb[:, c128(o, M)], yps[o], F.Copy) for o in range(3)]
     nump = ACT([num, c_pk], T.nump[:], T.num[:].indirect(T.pk[:]), F.Copy)
-    g3, e3, r3, oh3 = {}, {}, {}, {}
-    st3[0] = V([tS3[0], tie[0]], "ts", T.st3[:, 0:M], T.tie[:, 0:M], T.pss[:, 512:513], None, A.add)
-    for c in range(2):
-        g3[c] = V([tB3, tS3[c]], "ts", T.g3[lanes[c], c128(2 * c, M)], T.psb[lanes[c], 512:512 + M], T.pss[lanes[c], 512 * c + 512:512 * c + 513], None, A.is_gt)
-    for c in range(2):
+    ysb = [ACT([tY[o]], T.ysb[:, c128(o, M)], yps[o], F.Copy) for o in range(3)]
+    st3, g3, e3, r3, oh3 = {}, {}, {}, {}, {}
+    own = [T.pss[lanes[c], 512 * c + 512:512 * c + 513] for c in range(2)]
+
+    def first(c):
+        st3[c] = V([tS3[c], idr] + kp, "ts", T.st3[lanes[c], c128(c, M)], T.idr[lanes[c], :, 0:K2], T.kp[lanes[c], c:c + 1], own[c], A.add, A.max)
+
+    def larger(c):
+        g3[c] = V([tB3, tS3[c]], "ts", T.g3[lanes[c], c128(2 * c, M)], T.psb[lanes[c], 512:512 + M], own[c], None, A.is_gt)
+
+    def equal(c):
         e3[c] = V([st3[c]], "tt", T.g3[lanes[c], c128(2 * c + 1, M)], T.psb[lanes[c], 512:512 + M], T.st3[lanes[c], c128(c, M)], A.is_equal)
+
+    for step, c in ((first, 0), (larger, 0), (first, 1), (equal, 0), (larger, 1), (equal, 1)):
+        step(c)
     for c in range(2):
         r3[c] = V([g3[c], e3[c]], "scan", T.r3[lanes[c], c128(c, M)], T.g3[lanes[c], c128(2 * c, M)], T.g3[lanes[c], c128(2 * c + 1, M)], 0.0, A.add, A.add)
     for c in range(2):
         oh3[c] = V([r3[c]], "ts", T.oh3[lanes[c], c128(c, 256)], T.k3[lanes[c], :], T.r3[lanes[c], M * c + M - 1:M * c + M], T.j3[lanes[c], c:c + 1], A.is_equal, A.mult)
     t = [V([oh3[0]], "tr", T.ot3[0:64, :, 0:32], T.oh3[0:64, 0:256]), V([], "tr", T.ot3[0:64, :, 32:64], T.oh3[64:128, 0:256]),
          V([oh3[1]], "tr", T.ot3[0:32, :, 64:96], T.oh3[96:128, 256:512])]
-    off3 = lists(t, T.ot3, T.sm3, 8, T.off3)
+    t = sums(t, T.ot3, T.sm3, range(8))
+    off3 = [V(t, "copy", T.off3[p:p + 32, :], T.sm3[0:32, :, 95]) for p in (0, 32, 64, 96)]
     y0 = V(off3 + ysb, "copy", T.yo[:, c128(0)], T.ysb[:, c128(0, M)].indirect(T.off3[:]))
     y1 = ACT(off3 + ysb, T.yo[:, c128(1)], T.ysb[:, c128(1, M)].indirect(T.off3[:]), F.Copy)
     y2 = V([], "copy", T.yo[:, c128(2)], T.ysb[:, c128(2, M)].indirect(T.off3[:]))

@@ -8,22 +8,22 @@ SCRATCH = {"psb": ("psum", [128, 2048], "float32"), "pss": ("psum", [128, 2048],
            "tabd": ("dram", [N, 128, 1], "bfloat16"), "thop": ("dram", [128, 1], "bfloat16")}
 for _d, _l in (("float8_e4m3fn_x4", "xq 512 uq 128 ur 128 wq 384 snd1 128 land1 128 snd2 32 hq 20 land2 160"),
                ("uint8", "xs 512 us 128 urs 128 ws 384 snd1s 128 land1s 128 snd2s 32 hps 20 land2s 160"),
-               ("bfloat16", "xb 2048 ub 512 wb 1536 k2 192 k3 256 jb 4 j3 2 g1 2048 r1 1024 on2 256 mk2 256 g2 256"
+               ("bfloat16", "xb 2048 ub 512 wb 1536 k2 160 k3 256 jb 4 j3 2 g1 2048 r1 1024 on2 256 mk2 256 g2 256"
                 " g3 640 r3 320 oh3 512 u1 8 tab 1024 sg 384 sh 384"),
-               ("float16", "oh2 192"),
-               ("uint16", "zoff 8 off1 8 kb 2 koff 16 off3 8 pk 10"), ("int32", "pi 1 si 1 bi 1 ci 1 jq 10"),
+               ("float16", "oh2 160"),
+               ("uint16", "zoff 8 off0 2 off1 8 kb 2 koff 16 off3 8 pk 10"), ("int32", "pi 1 si 1 bi 1 ci 1 jq 10"),
                ("float32", "z32 32 zt 128 tri 128 ms 16 m0 16 m1 16 mk 18 sc1 4 st1 512 up1 4 ge1 1 r2 256 pf 1 p8 1 key 1"
-                " xr 256 kp 2 st3 320 ysb 480 yo 384 hk 4 num 256 pm 1 j16 10 jj 10 jr 10 nump 160 b256 1 ido 128")):
+                " xr 256 kp 2 st3 320 ysb 480 yo 384 hk 3 num 256 pm 1 j16 10 jj 10 jr 10 nump 160 b256 1 ido 128")):
     _w = _l.split()
     for _i in range(0, len(_w), 2):
         SCRATCH[_w[_i]] = ("sbuf", [128, int(_w[_i + 1])], _d)
 for _n, _k in (("krow", 32), ("krow3", 32), ("oh1", 128), ("ot1", 128), ("sm1", 128), ("ot3", 96), ("sm3", 96)):
     SCRATCH[_n] = ("sbuf", [128, 8, _k], "bfloat16")
-SCRATCH["ot2"] = ("sbuf", [128, 6, 64], "float16")
-SCRATCH["s2"] = ("sbuf", [128, 6, 64], "float32")
+SCRATCH["ot2"] = ("sbuf", [128, 5, 64], "float16")
+SCRATCH["s2"] = ("sbuf", [128, 5, 64], "float32")
 SCRATCH["idr"] = ("sbuf", [128, 8, 32], "float32")
 SCRATCH["kl"] = ("sbuf", [128, 8, 4], "float32")
-SEMAPHORES = "vec sca ten pool du dx0 dx1 dx2 dx3 dw a1 a2 ak at ht hx loc dt0 dt1 dy0 dy1 di".split()
+SEMAPHORES = "vec sca ten pool du dx0 dx1 dx2 dx3 dw a1 a2 ak at ha2 hak hat loc dt0 dt1 dy0 dy1 di".split()
 
 
 def helpers(r, T, topo):
@@ -31,11 +31,11 @@ def helpers(r, T, topo):
     free = sorted((h for h in topo.cores_of(core) if T.rank_of(h) is None), key=lambda h: (topo.die(h) != topo.die(core), h))
     wide = [h for h in free if all(topo.may_write(h, d) for d in T.cores)]
     plain = [h for h in free if h not in wide]
-    ring = [(r + b) % N for b in range(1, N + 1)]
+    ring = [(r + b) % N for b in range(1, N)]
     near = [d for d in ring if topo.may_write(plain[0], T.cores[d])]
     far = [d for d in ring if d not in near]
-    return [(wide[0], "keys", far, far), (plain[2], "keys", near[:-1], near[0:1]),
-            (plain[0], "codes", near, near[1:2]), (plain[1], "planes", near, near[2:3])]
+    return [(wide[0], [("keys", far[2:4]), ("planes", far)], far), (plain[1], [("planes", near + [r])], near[2:3]),
+            (plain[0], [("keys", near), ("codes", [near[2], r])], near[0:2])]
 
 
 def fused(g, T, topo, sem, engines, jobs, share=None):
@@ -45,7 +45,7 @@ def fused(g, T, topo, sem, engines, jobs, share=None):
         rid, pid = topo.addr(d)[0:2]
         mine = engines[sum(share[:i]):sum(share[:i + 1])]
         tr.append(RemoteDMATransfer(dst_ids=[DstId(rid=rid, pnc=pid)], dma_engine_mask=sum(1 << e for e in mine),
-                                    remote_sem=T.sem[sem], src=src, dst=dst))
+                                    remote_sem=T.sem[sem if T.rank_of(d) is not None else "h" + sem], src=src, dst=dst))
     g.remote_dma_fused(tr, local_sem=T.sem.loc)
     return sum(share)
 
@@ -56,14 +56,17 @@ def engines_of(core, T, topo):
     return off, [e for e in on if e not in off]
 
 
-def hand_on(g, core, r, what, to, tab_to, T, topo):
+def hand_on(g, core, r, what, tab_to, T, topo):
     off, on = engines_of(core, T, topo)
-    g.wait_ge(T.sem.ht, len(on) // 4)
+    g.wait_ge(T.sem.hat, 2)
     n = fused(g, T, topo, "at", off, [(T.cores[d], T.thop[:], T.tabd[r]) for d in tab_to])
-    g.wait_ge(T.sem.hx, len(on))
-    src, dst = {"planes": (T.hps[:], T.land2s[:, K2 * r:K2 * r + K2]), "keys": (T.hk[:], T.kl[:, r, :]),
-                "codes": (T.hq[:].bitcast(dt.uint8), T.land2[:, K2 * r:K2 * r + K2].bitcast(dt.uint8))}[what]
-    n += fused(g, T, topo, "ak" if what == "keys" else "a2", off, [(T.cores[d], src, dst) for d in to])
+    mine = slice(K2 * r, K2 * r + K2)
+    jobs = {"keys": ("ak", len(on), T.hk[:], T.kl[:, r, 0:3]), "planes": ("a2", len(on) // 2, T.hps[:], T.land2s[:, mine]),
+            "codes": ("a2", len(on), T.hq[:].bitcast(dt.uint8), T.land2[:, mine].bitcast(dt.uint8))}
+    for name, to in what:
+        sem, come, src, dst = jobs[name]
+        g.wait_ge(T.sem["h" + sem], come)
+        n += fused(g, T, topo, sem, off, [(T.cores[d], src, dst) for d in to])
     g.wait_ge(T.sem.loc, n)
 
 
@@ -71,9 +74,9 @@ def rank_program(g, core, T, topo):
     S, rank = T.sem, T.rank_of(core)
     if rank is None:
         for r in range(N):
-            for h, what, to, tab_to in helpers(r, T, topo):
+            for h, what, tab_to in helpers(r, T, topo):
                 if h == core:
-                    hand_on(g, core, r, what, to, tab_to, T, topo)
+                    hand_on(g, core, r, what, tab_to, T, topo)
         return
     q = {"vec": g.vector, "sca": g.scalar, "ten": g.tensor, "pool": g, "sync": g.sync}
     v = g.vector
@@ -151,20 +154,20 @@ def rank_program(g, core, T, topo):
     P(T.mk2[:], T.on2[:], [[-1, 256]], A.not_equal, 0.0, 0, 1)
     IOTA(T.pf[:], [[0, 1]], 0, 1)
     c_p8 = IOTA(T.p8[:], [[0, 1]], 0, 8)
-    IOTA(T.k2[:, 128:160], [[1, 32]], 0, 0)
+    IOTA(T.k2[:, 0:64], [[16, 2], [0, 2], [1, 16]], 0, 0)
+    IOTA(T.k2[:, 64:96], [[1, 32]], 0, 0)
+    IOTA(T.k2[:, 96:128], [[0, 2], [1, 16]], 16, 0)
     sh = K2 * rank % 32
-    IOTA(T.k2[:, 160 + sh:192], [[1, 32 - sh]], 0, 0)
+    IOTA(T.k2[:, 128 + sh:160], [[1, 32 - sh]], 0, 0)
     if sh:
-        IOTA(T.k2[:, 160:160 + sh], [[1, sh]], 32 - sh, 0)
-    for a in (0, 64):
-        IOTA(T.k2[:, a:a + 64], [[16, 2], [0, 2], [1, 16]], 0, 0)
+        IOTA(T.k2[:, 128:128 + sh], [[1, sh]], 32 - sh, 0)
     c_k2 = IOTA(T.j16[:], [[16, M // 16]], 0, 1)
 
     qu = V([du, c_ub], "qz", T.uq[:], T.us[:], T.ub[:])
     c_us = ACT([qu, c_zoff], T.urs[:], T.us[:].indirect(T.zoff[:]), F.Copy)
     U = (T.ur[:], T.urs[:])
 
-    tq, tS, tB, sc, up, st, rk, oh, tr, last = [{} for _ in range(10)]
+    tq, tS, tB, sc, up, st, rk, oh, last = [{} for _ in range(9)]
 
     def quant(i):
         tq[i] = V([dx[i]], "qz", T.xq[:, c128(i)], T.xs[:, c128(i)], T.xb[:, c128(i, 512)])
@@ -193,11 +196,12 @@ def rank_program(g, core, T, topo):
         else:
             rk[c] = V([last[c], ge], "scan", T.r1[:, 896:1024], T.g1[:, 1920:2048], T.g1[:, 1920:2048], T.ge1[:], A.add, A.add)
 
-    def onehot(c):
-        oh[c] = V([rk[c], c_kr], "ts", T.oh1[:, :, c128(c, 32)], (T.krow3 if c == 3 else T.krow)[:], T.r1[:, 256 * c + 255:256 * c + 256], T.jb[:, c:c + 1], A.is_equal, A.mult)
+    def onehot(c, b=slice(0, 8)):
+        oh[c] = V([rk[c], c_kr], "ts", T.oh1[:, b, c128(c, 32)], (T.krow3 if c == 3 else T.krow)[:, b, :], T.r1[:, 256 * c + 255:256 * c + 256], T.jb[:, c:c + 1], A.is_equal, A.mult)
+        return oh[c]
 
-    def turn(c):
-        tr[c] = V([oh[c]], "tr", T.ot1[:, :, c128(c, 32)], T.oh1[:, :, c128(c, 32)])
+    def turn(c, b=slice(0, 8), tok=None):
+        return V([tok or oh[c]], "tr", T.ot1[:, b, c128(c, 32)], T.oh1[:, b, c128(c, 32)])
 
     quant(0)
     quant(1)
@@ -228,16 +232,44 @@ def rank_program(g, core, T, topo):
     count(3)
     turn(0)
     onehot(2)
-    onehot(3)
-    for c in (1, 2, 3):
-        turn(c)
+    H = (slice(7, 8), slice(4, 7), slice(0, 4))
+    lists = (T.off0[:, 0:1], T.off1[:, H[1]], T.off1[:, H[2]])
+    o3 = [onehot(3, H[0]), onehot(3, slice(0, 7))]
+    turn(1)
+    turn(3, H[0], o3[0])
+    t = turn(2, H[0])
+    turn(2, slice(0, 7))
+    rest = turn(3, slice(0, 7), o3[1])
     free1 = [last[3], sg]
-    sm = [V([tr[3]], "scan", T.sm1[0:64, b, :], T.ot1[0:64, b, :], T.ot1[64:128, b, :], 0.0, A.add, A.add) for b in range(8)]
-    l1 = [V(sm, "tt", T.u1[p:p + 32, :], T.sm1[0:32, :, 127], T.sm1[32:64, :, 127], A.add) for p in (0, 32)]
-    off1 = [V(l1, "ts", T.off1[p:p + 64, :], T.u1[0:64, :], 256.0, None, A.add) for p in (0, 64)]
+
+    def halves(a, tok):
+        return [V([tok], "scan", T.sm1[0:64, b, :], T.ot1[0:64, b, :], T.ot1[64:128, b, :], 0.0, A.add, A.add) for b in range(N)[H[a]]]
+
+    def numbers(toks, h):
+        return [V(toks, "tt", T.u1[p:p + 32, h], T.sm1[0:32, h, 127], T.sm1[32:64, h, 127], A.add) for p in (0, 32)]
+
+    def offsets(toks, h):
+        return [V(toks, "ts", T.off1[p:p + 64, h], T.u1[0:64, h], 256.0, None, A.add) for p in (0, 64)]
+
+    def pick_codes(a, toks):
+        return V(toks, "copy", u32(T.snd1[:, NB * H[a].start:NB * H[a].stop]), u32(T.xq[:]).indirect(lists[a]))
+
+    def pick_planes(a, toks):
+        return ACT(toks, T.snd1s[:, NB * H[a].start:NB * H[a].stop], T.xs[:].indirect(lists[a]), F.Copy)
+
+    t = halves(0, t)
+    t = [V(t, "ts", T.off0[p:p + 32, 0:1], T.sm1[0:32, 7, 127:128], T.sm1[32:64, 7, 127:128], 256.0, A.add, A.add) for p in (0, 32, 64, 96)]
+    pp = [pick_planes(0, t)]
+    sm = [halves(1, rest), halves(2, rest)]
+    t = offsets(numbers(sm[0], slice(4, 8)), H[1])
+    pp.append(pick_planes(1, t))
+    l1 = numbers(sm[1], H[2])
+    pick_codes(0, l1)
+    pc = [pick_codes(1, [])]
+    t = offsets(l1, H[2])
+    pp.append(pick_planes(2, t))
+    pc.append(pick_codes(2, t))
     me1 = c128(rank, NB)
-    pc = V(off1, "copy", u32(T.snd1[:]), u32(T.xq[:]).indirect(T.off1[:]))
-    psc = ACT(off1, T.snd1s[:], T.xs[:].indirect(T.off1[:]), F.Copy)
     oc = V([], "copy", u32(T.land1[:, me1]), u32(T.xq[:]).indirect(T.off1[:, 0:1]))
     osc = ACT([], T.land1s[:, me1], T.xs[:].indirect(T.off1[:, 0:1]), F.Copy)
     dt0 = dma("sync", l1, T.tabd[rank], T.u1[0:16, :], "dt0")
@@ -245,23 +277,22 @@ def rank_program(g, core, T, topo):
     off, on = engines_of(core, T, topo)
     hs = helpers(rank, T, topo)
     ring = [T.cores[(rank + b) % N] for b in range(1, N)]
-    need("pool", [pc])
     codes = [(ring[b - 1], u8(T.snd1[:, c128(b, NB)]), u8(T.land1[:, me1])) for b in range(1, N)]
     planes = [(ring[b - 1], T.snd1s[:, c128(b, NB)], T.land1s[:, me1]) for b in range(1, N)]
-    loc = fused(g, T, topo, "a1", off, codes[0::2])
-    need("pool", [psc])
-    loc += fused(g, T, topo, "a1", off, planes[0::2])
-    loc += fused(g, T, topo, "a1", off, codes[1::2], (4, 2, 2))
-    loc += fused(g, T, topo, "a1", off, planes[1::2], (2, 2, 4))
+    loc = 0
+    for tok, jobs, share in ((pp[0], planes[6:7], None), (pp[1], planes[3:6], (2, 2, 4)), (pc[0], codes[3:7], None),
+                             (pp[2], planes[0:2], None), (pc[1], codes[0:3], (4, 2, 2)), (pc[1], planes[2:3], None)):
+        need("pool", [tok])
+        loc += fused(g, T, topo, "a1", off, jobs, share)
     loc1 = loc
+    need("pool", [dt0])
+    loc += fused(g, T, topo, "at", on, [(h[0], T.tabd[rank], T.thop[:]) for h in hs])
     t = P(T.m0[:], T.ms[:], [[32, 2], [-K2, 8]], A.is_ge, 0.0, 0, 1)
     IOTA(T.k3[:], [[16, 8], [0, 2], [1, 16]], 0, 0)
     IOTA(T.j3[:], [[32, 2]], 0, 1)
     IOTA(T.b256[:], [[0, 1]], 0, 256)
     need("pool", [t])
     c_k3 = P(T.m1[:], T.m0[:], [[-32, 2], [K2, 8]], A.is_ge, 0.0, K2 - 1, -1)
-    need("pool", [dt0])
-    loc += fused(g, T, topo, "ht", on, [(h[0], T.tabd[rank], T.thop[:]) for h in hs])
 
     wq = V([dw], "qz", T.wq[:], T.ws[:], T.wb[:])
     t = V([c_pi], "ts", T.si[:], T.pi[:], 4, None, A.arith_shift_right)
@@ -283,41 +314,48 @@ def rank_program(g, core, T, topo):
     V([tB2], "ts", T.g2[:, 0:128], T.psb[:, 0:128], T.pss[:, 0:1], -1.0, A.is_equal, A.mult)
     e2 = V([], "ts", T.g2[:, 128:256], T.psb[:, 0:128], T.pss[:, 0:1], None, A.is_ge)
     r2 = V([e2], "scan", T.r2[:], T.mk2[:], T.g2[:], 0.0, A.mult, A.add)
-    tk = V([r2, c_key], "ts", T.oh2[:, 64:192], T.k2[:, 64:192], T.r2[:, 255:256], T.key[:], A.is_equal, A.mult)
+    tk = V([r2, c_key], "ts", T.oh2[:, 64:160], T.k2[:, 64:160], T.r2[:, 255:256], T.key[:], A.is_equal, A.mult)
     tp = V([], "ts", T.oh2[:, 0:64], T.k2[:, 0:64], T.r2[:, 255:256], T.pf[:], A.is_equal, A.mult)
-    tk = [V([tk], "tr", T.ot2[0:64, 2:6, c128(a, 32)], T.oh2[c128(a, 64), 64:192]) for a in range(2)]
+    tk = [V([tk], "tr", T.ot2[0:64, 2:5, c128(a, 32)], T.oh2[c128(a, 64), 64:160]) for a in range(2)]
     tp = [V([tp], "tr", T.ot2[0:64, 0:2, c128(a, 32)], T.oh2[c128(a, 64), 0:64]) for a in range(2)]
-    tk = sums(tk, T.ot2, T.s2, range(2, 6))
+    tk = sums(tk, T.ot2, T.s2, range(2, 5))
     tp = sums(tp, T.ot2, T.s2, range(2))
-    ks = [V(tp, "ts", T.kl[p:p + 32, rank, :], T.s2[0:32, 2:6, 63], KS, None, A.mult) for p in (0, 32)]
-    ks += [ACT(tk, T.kl[p:p + 32, rank, :], T.s2[0:32, 2:6, 63], F.Identity, scale=KS) for p in (64, 96)]
+    ks = [ACT(tk, T.kl[p:p + 32, rank, 0:3], T.s2[0:32, 2:5, 63], F.Identity, scale=KS) for p in (0, 32, 64, 96)]
     off2 = [V(tp, "copy", T.kb[p:p + 32, :], T.s2[0:32, 0:2, 63]) for p in (0, 32, 64, 96)]
     me2 = c128(rank, K2)
     pc = V(off2 + arr1, "copy", u32(T.snd2[:, 0:32]), u32(T.land1[:]).indirect(T.kb[:, 0:2]))
     psc = ACT(off2 + arr1, T.snd2s[:, 0:32], T.land1s[:].indirect(T.kb[:, 0:2]), F.Copy)
     need("pool", ks)
-    loc += fused(g, T, topo, "hx", off + on, [(h[0], T.kl[:, rank, :], T.hk[:]) for h in hs[0:2]])
-    far = [T.cores[d] for d in hs[0][2]]
-    need("pool", [pc])
-    loc += fused(g, T, topo, "hx", on, [(hs[2][0], u8(T.snd2[:, 0:K2]), u8(T.hq[:]))])
-    loc += fused(g, T, topo, "a2", off, [(d, u8(T.snd2[:, 0:K2]), u8(T.land2[:, me2])) for d in far])
+    far, near = [T.cores[d] for d in hs[0][2]], [T.cores[d] for d in hs[2][2]]
+    keys = T.kl[:, rank, 0:3]
+    loc += fused(g, T, topo, "ak", off + on, [(d, keys, keys) for d in far[0:2]] + [(hs[2][0], keys, T.hk[:])], (4, 4, 8))
+    loc += fused(g, T, topo, "ak", on, [(hs[0][0], keys, T.hk[:])])
+    codes, planes = (u8(T.snd2[:, 0:K2]), u8(T.land2[:, me2])), (T.snd2s[:, 0:K2], T.land2s[:, me2])
     need("pool", [psc])
-    loc += fused(g, T, topo, "hx", on, [(hs[3][0], T.snd2s[:, 0:K2], T.hps[:])])
-    loc += fused(g, T, topo, "a2", off, [(d, T.snd2s[:, 0:K2], T.land2s[:, me2]) for d in far])
-    at = ("at", sum(len(off) // len(h[3]) for r in range(N) for h in helpers(r, T, topo) if rank in h[3]))
+    loc += fused(g, T, topo, "a2", on, [(h[0], planes[0], T.hps[:]) for h in hs[0:2]])
+    need("pool", [pc])
+    loc += fused(g, T, topo, "a2", on, [(hs[2][0], codes[0], u8(T.hq[:]))])
+    loc += fused(g, T, topo, "a2", off, [(d,) + codes for d in far])
+    loc += fused(g, T, topo, "a2", off, [(d,) + codes for d in near])
+    at = ("at", len(off) * len(hs))
     dt1 = dma("sync", [at, dt0, c_tab], T.tab[1:2, :], T.tabd[:], "dt1")
 
-    ak = ("ak", 2 * (N - 1))
-    xr = [ACT([ak] + ks, T.xr[:, c128(b, 32)], T.z32[:], F.Identity, bias=T.kl[:, b, 2:3]) for b in range(3)]
-    xr += [V([ak, c_k3] + ks, "ts", T.xr[:, c128(b, 32)], T.z32[:], T.kl[:, b, 2:3], None, A.add) for b in range(3, 8)]
-    t = [V([], "tt", T.mk[:, 9 * c:9 * c + 8], T.kl[:, :, 3], T.m1[:, c128(c, 8)], A.mult) for c in range(2)]
-    koff = V([], "ts", T.koff[:], T.kl[:, :, 0:2], 1.0 / KS, None, A.mult)
-    idr = V(xr, "tr", T.idr[:], T.xr[:])
+    ak = ("ak", 4 * len(far) + 2 * (N - 1 - len(far)))
+    xr, order = {}, [rank] + [b for b in range(N) if b != rank]
+    for i, b in enumerate(order):
+        if i < 5:
+            xr[b] = V(([ak] if i else [c_k3]) + ks, "ts", T.xr[:, c128(b, 32)], T.z32[:], T.kl[:, b, 0:1], None, A.add)
+        else:
+            xr[b] = ACT([ak], T.xr[:, c128(b, 32)], T.z32[:], F.Identity, bias=T.kl[:, b, 0:1])
+    t = [V([], "tt", T.mk[:, 9 * c:9 * c + 8], T.kl[:, :, 2], T.m1[:, c128(c, 8)], A.mult) for c in range(2)]
+    V([xr[b] for b in range(4)], "tr", T.idr[:, 0:4, :], T.xr[:, 0:128])
+    idr = V([xr[b] for b in range(4, 8)], "tr", T.idr[:, 4:8, :], T.xr[:, 128:256])
     kp = [V([t[c]], "red", T.kp[:, c:c + 1], T.mk[:, c128(c, 9)], AxisListType.X, A.add) for c in range(2)]
+    koff = V([], "ts", T.koff[:], T.kl[:, :, 0:2], 1.0 / KS, None, A.mult)
     num = ACT([koff, dt1], T.num[:], T.tab[:].indirect(T.koff[:]), F.Copy)
     lanes = (slice(0, 128), slice(96, 128))
 
-    arr2 = [("a2", 4 * N)]
+    arr2 = [("a2", 5 * len(off))]
     L2 = (T.land2[:], T.land2s[:])
     tS3 = [MM(arr2 + [e2] + free1, T.pss[:, 512:640], (T.land2[:, 0:128], T.land2s[:, 0:128]), U)]
     tB3 = MM([], T.psb[:, 512:512 + M], U, L2)
@@ -342,11 +380,16 @@ def rank_program(g, core, T, topo):
         step(c)
     for c in range(2):
         r3[c] = V([g3[c], e3[c]], "scan", T.r3[lanes[c], c128(c, M)], T.g3[lanes[c], c128(2 * c, M)], T.g3[lanes[c], c128(2 * c + 1, M)], 0.0, A.add, A.add)
-    for c in range(2):
-        oh3[c] = V([r3[c]], "ts", T.oh3[lanes[c], c128(c, 256)], T.k3[lanes[c], :], T.r3[lanes[c], M * c + M - 1:M * c + M], T.j3[lanes[c], c:c + 1], A.is_equal, A.mult)
-    t = [V([oh3[0]], "tr", T.ot3[0:64, :, 0:32], T.oh3[0:64, 0:256]), V([], "tr", T.ot3[0:64, :, 32:64], T.oh3[64:128, 0:256]),
-         V([oh3[1]], "tr", T.ot3[0:32, :, 64:96], T.oh3[96:128, 256:512])]
-    t = sums(t, T.ot3, T.sm3, range(8))
+    for c, a, n in ((0, 0, 256), (1, 0, 128), (1, 128, 128)):
+        oh3[c, a] = V([r3[c]], "ts", T.oh3[lanes[c], 256 * c + a:256 * c + a + n], T.k3[lanes[c], a:a + n], T.r3[lanes[c], M * c + M - 1:M * c + M],
+                      T.j3[lanes[c], c:c + 1], A.is_equal, A.mult)
+    V([oh3[0, 0]], "tr", T.ot3[0:64, 0:4, 0:32], T.oh3[0:64, 0:128])
+    V([], "tr", T.ot3[0:64, 0:4, 32:64], T.oh3[64:128, 0:128])
+    V([], "tr", T.ot3[0:64, 4:8, 0:32], T.oh3[0:64, 128:256])
+    ta = V([oh3[1, 0]], "tr", T.ot3[0:32, 0:4, 64:96], T.oh3[96:128, 256:384])
+    V([], "tr", T.ot3[0:64, 4:8, 32:64], T.oh3[64:128, 128:256])
+    tb = V([oh3[1, 128]], "tr", T.ot3[0:32, 4:8, 64:96], T.oh3[96:128, 384:512])
+    t = sums([ta], T.ot3, T.sm3, range(4)) + sums([tb], T.ot3, T.sm3, range(4, 8))
     off3 = [V(t, "copy", T.off3[p:p + 32, :], T.sm3[0:32, :, 95]) for p in (0, 32, 64, 96)]
     y0 = V(off3 + ysb, "copy", T.yo[:, c128(0)], T.ysb[:, c128(0, M)].indirect(T.off3[:]))
     y1 = ACT(off3 + ysb, T.yo[:, c128(1)], T.ysb[:, c128(1, M)].indirect(T.off3[:]), F.Copy)

from concourse.bass import DstId, RemoteDMATransfer
from concourse.mybir import dt, AluOpType as A, ActivationFunctionType as F, AxisListType

N, NB, K2, KS = 8, 16, 20, 2.0 ** 80
STEP, TINY = 0.625 * 2.0 ** -23, 2.0 ** -124
M = N * K2
SCRATCH = {"psb": ("psum", [128, 2048], "float32"), "pss": ("psum", [128, 2048], "float32"),
           "tabd": ("dram", [N, 128, 1], "bfloat16"), "thop": ("dram", [128, 1], "bfloat16")}
for _d, _l in (("float8_e4m3fn_x4", "xq 512 uq 128 ur 128 wq 384 snd1 128 land1 128 snd2 32 hq 20 land2 160"),
               ("uint8", "xs 512 us 128 urs 128 ws 384 snd1s 128 land1s 128 snd2s 32 hps 20 land2s 160"),
               ("bfloat16", "xb 2048 ub 512 wb 1536 k2 160 k3 256 jb 4 j3 2 g1 2048 r1 1024 on2 256 mk2 256 g2 256"
                " g3 640 r3 320 oh3 512 u1 8 tab 1024 sg 384 sh 384"),
               ("float16", "oh2 160"),
               ("uint16", "zoff 8 off0 2 off1 8 kb 2 koff 16 off3 8 pk 10"), ("int32", "pi 1 si 1 bi 1 ci 1 jq 10"),
               ("float32", "z32 32 zt 128 tri 128 ms 16 m0 16 m1 16 mk 18 sc1 4 st1 512 up1 4 ge1 1 r2 256 pf 1 p8 1 key 1"
                " xr 256 kp 2 st3 320 ysb 480 yo 384 hk 3 num 256 pm 1 j16 10 jj 10 jr 10 nump 160 b256 1 ido 128")):
    _w = _l.split()
    for _i in range(0, len(_w), 2):
        SCRATCH[_w[_i]] = ("sbuf", [128, int(_w[_i + 1])], _d)
for _n, _k in (("krow", 32), ("krow3", 32), ("oh1", 128), ("ot1", 128), ("sm1", 128), ("ot3", 96), ("sm3", 96)):
    SCRATCH[_n] = ("sbuf", [128, 8, _k], "bfloat16")
SCRATCH["ot2"] = ("sbuf", [128, 5, 64], "float16")
SCRATCH["s2"] = ("sbuf", [128, 5, 64], "float32")
SCRATCH["idr"] = ("sbuf", [128, 8, 32], "float32")
SCRATCH["kl"] = ("sbuf", [128, 8, 4], "float32")
SEMAPHORES = "vec sca ten pool du dx0 dx1 dx2 dx3 dw a1 a2 ak at ha2 hak hat loc dt0 dt1 dy0 dy1 di".split()


def helpers(r, T, topo):
    core = T.cores[r]
    free = sorted((h for h in topo.cores_of(core) if T.rank_of(h) is None), key=lambda h: (topo.die(h) != topo.die(core), h))
    wide = [h for h in free if all(topo.may_write(h, d) for d in T.cores)]
    plain = [h for h in free if h not in wide]
    ring = [(r + b) % N for b in range(1, N)]
    near = [d for d in ring if topo.may_write(plain[0], T.cores[d])]
    far = [d for d in ring if d not in near]
    return [(wide[0], [("keys", far[2:4]), ("planes", far)], far), (plain[1], [("planes", near + [r])], near[2:3]),
            (plain[0], [("keys", near), ("codes", [near[2], r])], near[0:2])]


def fused(g, T, topo, sem, engines, jobs, share=None):
    share = share or [len(engines) // len(jobs)] * len(jobs)
    tr = []
    for i, (d, src, dst) in enumerate(jobs):
        rid, pid = topo.addr(d)[0:2]
        mine = engines[sum(share[:i]):sum(share[:i + 1])]
        tr.append(RemoteDMATransfer(dst_ids=[DstId(rid=rid, pnc=pid)], dma_engine_mask=sum(1 << e for e in mine),
                                    remote_sem=T.sem[sem if T.rank_of(d) is not None else "h" + sem], src=src, dst=dst))
    g.remote_dma_fused(tr, local_sem=T.sem.loc)
    return sum(share)


def engines_of(core, T, topo):
    off = topo.engines(core, [d for d in T.cores if topo.chip(d) != topo.chip(core) and topo.may_write(core, d)][0])
    on = topo.engines(core, [h for h in topo.cores_of(core) if h != core][0])
    return off, [e for e in on if e not in off]


def hand_on(g, core, r, what, tab_to, T, topo):
    off, on = engines_of(core, T, topo)
    g.wait_ge(T.sem.hat, 2)
    n = fused(g, T, topo, "at", off, [(T.cores[d], T.thop[:], T.tabd[r]) for d in tab_to])
    mine = slice(K2 * r, K2 * r + K2)
    jobs = {"keys": ("ak", len(on), T.hk[:], T.kl[:, r, 0:3]), "planes": ("a2", len(on) // 2, T.hps[:], T.land2s[:, mine]),
            "codes": ("a2", len(on), T.hq[:].bitcast(dt.uint8), T.land2[:, mine].bitcast(dt.uint8))}
    for name, to in what:
        sem, come, src, dst = jobs[name]
        g.wait_ge(T.sem["h" + sem], come)
        n += fused(g, T, topo, sem, off, [(T.cores[d], src, dst) for d in to])
    g.wait_ge(T.sem.loc, n)


def rank_program(g, core, T, topo):
    S, rank = T.sem, T.rank_of(core)
    if rank is None:
        for r in range(N):
            for h, what, tab_to in helpers(r, T, topo):
                if h == core:
                    hand_on(g, core, r, what, tab_to, T, topo)
        return
    q = {"vec": g.vector, "sca": g.scalar, "ten": g.tensor, "pool": g, "sync": g.sync}
    v = g.vector
    ops = {"copy": v.tensor_copy, "tt": v.tensor_tensor, "ts": v.tensor_scalar, "red": v.tensor_reduce, "scan": v.tensor_tensor_scan,
           "tr": v.transpose, "set": v.memset, "qz": v.quantize_mx}
    cnt, seen = {}, {}

    def need(e, toks):
        best = {}
        for s, n in toks:
            best[s] = max(best.get(s, 0), n)
        for s in best:
            if seen.get((e, s), 0) < best[s]:
                q[e].wait_ge(S[s], best[s])
                seen[(e, s)] = best[s]

    def done(e, ins):
        cnt[e] = cnt.get(e, 0) + 1
        ins.then_inc(S[e], 1)
        return (e, cnt[e])

    def V(toks, name, *a):
        need("vec", toks)
        return done("vec", ops[name](*a))

    def ACT(toks, *a, **k):
        need("sca", toks)
        return done("sca", g.scalar.activation(*a, **k))

    def MM(toks, out, l, r):
        need("ten", toks)
        return done("ten", g.tensor.matmul_mx(out, l[0], l[1], r[0], r[1], True, True))

    def P(*a):
        return done("pool", g.affine_select(*a))

    def IOTA(*a):
        return done("pool", g.iota(*a, allow_small_or_imprecise_dtypes=True))

    def dma(e, toks, out, in_, sem):
        need(e, toks)
        q[e].dma_start(out, in_).then_inc(S[sem], 16)
        return (sem, 16)

    def u32(ap):
        return ap.bitcast(dt.uint32)

    def u8(ap):
        return ap.bitcast(dt.uint8)

    def c128(i, w=128):
        return slice(w * i, w * i + w)

    def sums(toks, ot, sm, blocks):
        return [V(toks, "scan", sm[0:32, b, :], ot[0:32, b, :], ot[32:64, b, :], 0.0, A.add, A.add) for b in blocks]

    du = dma("sca", [], T.ub[:, 0:8], T.u[:, 0:8], "du")
    dx = [dma("sync", [], T.xb[:, c128(i, 512)], T.x[:, c128(i, 512)], "dx%d" % i) for i in range(4)]
    dw = dma("sync", [dx[3]], T.wb[:], T.w[:], "dw")

    c_ub = V([], "set", T.ub[:, 8:512], 0.0)
    c_zoff = V([], "set", T.zoff[:], 0)
    c_zt = V([], "set", T.zt[:], 0.0)
    V([], "set", T.ms[:], -1.0)
    c_on = V([], "set", T.on2[:], 1.0)
    V([], "set", T.z32[:], 0.0)
    V([], "set", T.mk[:, 8:18:9], 0.5 * KS)
    V([], "set", T.ot3[32:64, :, 64:96], 0.0)
    c_pi = done("pool", g.iota(T.pi[:], [[0, 1]], 0, 1))
    need("pool", [c_zt, c_on])
    c_tri = P(T.tri[:], T.zt[:], [[-1, 128]], A.is_gt, 1.0, 0, 1)
    IOTA(T.jb[:], [[128, 4]], -256, 1)
    IOTA(T.krow[:], [[1, 8], [0, 2], [8, 16]], 0, 0)
    c_kr = IOTA(T.krow3[:], [[2, 8], [0, 2], [16, 16]], -384, 0)
    P(T.mk2[:], T.on2[:], [[-1, 256]], A.not_equal, 0.0, 0, 1)
    IOTA(T.pf[:], [[0, 1]], 0, 1)
    c_p8 = IOTA(T.p8[:], [[0, 1]], 0, 8)
    IOTA(T.k2[:, 0:64], [[16, 2], [0, 2], [1, 16]], 0, 0)
    IOTA(T.k2[:, 64:96], [[1, 32]], 0, 0)
    IOTA(T.k2[:, 96:128], [[0, 2], [1, 16]], 16, 0)
    sh = K2 * rank % 32
    IOTA(T.k2[:, 128 + sh:160], [[1, 32 - sh]], 0, 0)
    if sh:
        IOTA(T.k2[:, 128:128 + sh], [[1, sh]], 32 - sh, 0)
    c_k2 = IOTA(T.j16[:], [[16, M // 16]], 0, 1)

    qu = V([du, c_ub], "qz", T.uq[:], T.us[:], T.ub[:])
    c_us = ACT([qu, c_zoff], T.urs[:], T.us[:].indirect(T.zoff[:]), F.Copy)
    U = (T.ur[:], T.urs[:])

    tq, tS, tB, sc, up, st, rk, oh, last = [{} for _ in range(9)]

    def quant(i):
        tq[i] = V([dx[i]], "qz", T.xq[:, c128(i)], T.xs[:, c128(i)], T.xb[:, c128(i, 512)])

    def lane(i):
        tS[i] = MM([tq[i]], T.pss[:, 512 * i:512 * i + 128], (T.xq[:, c128(i)], T.xs[:, c128(i)]), (T.uq[:], T.us[:]))

    def score(i):
        sc[i] = ACT([tS[i]], T.sc1[:, i:i + 1], T.pss[:, 512 * i:512 * i + 1], F.Copy)
        up[i] = ACT([], T.up1[:, i:i + 1], T.pss[:, 512 * i:512 * i + 1], F.Abs, bias=TINY, scale=STEP)

    def level(i):
        st[i] = ACT([up[i], c_tri], T.st1[:, c128(i)], T.tri[:], F.Identity, bias=T.sc1[:, i:i + 1], scale=T.up1[:, i:i + 1])

    def blocks(*ci):
        for c, i in ci:
            out, s = T.g1[:, 512 * c + 128 * i:512 * c + 128 * i + 128], T.psb[:, 512 * i:512 * i + 128]
            if i == c:
                last[c] = V([tB[c], st[c]], "tt", out, s, T.st1[:, c128(c)], A.is_ge)
            else:
                last[c] = V([tB[i], sc[c]], "ts", out, s, T.sc1[:, c:c + 1], None, A.is_ge if i < c else A.is_gt)

    def count(c):
        if c < 3:
            rk[c] = V([last[c]], "scan", T.r1[:, c128(c, 256)], T.g1[:, 512 * c:512 * c + 256], T.g1[:, 512 * c + 256:512 * c + 512], 0.0, A.add, A.add)
        else:
            rk[c] = V([last[c], ge], "scan", T.r1[:, 896:1024], T.g1[:, 1920:2048], T.g1[:, 1920:2048], T.ge1[:], A.add, A.add)

    def onehot(c, b=slice(0, 8)):
        oh[c] = V([rk[c], c_kr], "ts", T.oh1[:, b, c128(c, 32)], (T.krow3 if c == 3 else T.krow)[:, b, :], T.r1[:, 256 * c + 255:256 * c + 256], T.jb[:, c:c + 1], A.is_equal, A.mult)
        return oh[c]

    def turn(c, b=slice(0, 8), tok=None):
        return V([tok or oh[c]], "tr", T.ot1[:, b, c128(c, 32)], T.oh1[:, b, c128(c, 32)])

    quant(0)
    quant(1)
    c_ur = V([qu, c_zoff], "copy", u32(T.ur[:]), u32(T.uq[:]).indirect(T.zoff[:]))
    quant(2)
    quant(3)
    for i in range(4):
        if i != 1:
            lane(i)
        if i == 0:
            lane(1)
        tB[i] = MM([c_ur, c_us], T.psb[:, 512 * i:512 * i + 128], U, (T.xq[:, c128(i)], T.xs[:, c128(i)]))
        score(i)
        if i:
            level(i - 1)
    t = MM([up[0]], T.pss[:, 0:384], U, (T.xq[:, 0:384], T.xs[:, 0:384]))
    sg = ACT([t, sc[3]], T.sg[:], T.pss[:, 0:384], F.Sign, bias=T.sc1[:, 3:4], scale=-1.0)
    level(3)
    ge = ACT([sg], T.sh[:], T.sg[:], F.Sign, bias=0.5, scale=-1.0, accum_out=T.ge1[:])
    blocks((1, 0), (0, 1), (0, 0), (1, 2), (0, 2), (2, 0), (0, 3), (1, 1), (2, 1), (1, 3))
    count(0)
    blocks((2, 3), (2, 2))
    count(1)
    onehot(0)
    blocks((3, 3))
    count(2)
    onehot(1)
    count(3)
    turn(0)
    onehot(2)
    H = (slice(7, 8), slice(4, 7), slice(0, 4))
    lists = (T.off0[:, 0:1], T.off1[:, H[1]], T.off1[:, H[2]])
    o3 = [onehot(3, H[0]), onehot(3, slice(0, 7))]
    turn(1)
    turn(3, H[0], o3[0])
    t = turn(2, H[0])
    turn(2, slice(0, 7))
    rest = turn(3, slice(0, 7), o3[1])
    free1 = [last[3], sg]

    def halves(a, tok):
        return [V([tok], "scan", T.sm1[0:64, b, :], T.ot1[0:64, b, :], T.ot1[64:128, b, :], 0.0, A.add, A.add) for b in range(N)[H[a]]]

    def numbers(toks, h):
        return [V(toks, "tt", T.u1[p:p + 32, h], T.sm1[0:32, h, 127], T.sm1[32:64, h, 127], A.add) for p in (0, 32)]

    def offsets(toks, h):
        return [V(toks, "ts", T.off1[p:p + 64, h], T.u1[0:64, h], 256.0, None, A.add) for p in (0, 64)]

    def pick_codes(a, toks):
        return V(toks, "copy", u32(T.snd1[:, NB * H[a].start:NB * H[a].stop]), u32(T.xq[:]).indirect(lists[a]))

    def pick_planes(a, toks):
        return ACT(toks, T.snd1s[:, NB * H[a].start:NB * H[a].stop], T.xs[:].indirect(lists[a]), F.Copy)

    t = halves(0, t)
    t = [V(t, "ts", T.off0[p:p + 32, 0:1], T.sm1[0:32, 7, 127:128], T.sm1[32:64, 7, 127:128], 256.0, A.add, A.add) for p in (0, 32, 64, 96)]
    pp = [pick_planes(0, t)]
    sm = [halves(1, rest), halves(2, rest)]
    t = offsets(numbers(sm[0], slice(4, 8)), H[1])
    pp.append(pick_planes(1, t))
    l1 = numbers(sm[1], H[2])
    pick_codes(0, l1)
    pc = [pick_codes(1, [])]
    t = offsets(l1, H[2])
    pp.append(pick_planes(2, t))
    pc.append(pick_codes(2, t))
    me1 = c128(rank, NB)
    oc = V([], "copy", u32(T.land1[:, me1]), u32(T.xq[:]).indirect(T.off1[:, 0:1]))
    osc = ACT([], T.land1s[:, me1], T.xs[:].indirect(T.off1[:, 0:1]), F.Copy)
    dt0 = dma("sync", l1, T.tabd[rank], T.u1[0:16, :], "dt0")

    off, on = engines_of(core, T, topo)
    hs = helpers(rank, T, topo)
    ring = [T.cores[(rank + b) % N] for b in range(1, N)]
    codes = [(ring[b - 1], u8(T.snd1[:, c128(b, NB)]), u8(T.land1[:, me1])) for b in range(1, N)]
    planes = [(ring[b - 1], T.snd1s[:, c128(b, NB)], T.land1s[:, me1]) for b in range(1, N)]
    loc = 0
    for tok, jobs, share in ((pp[0], planes[6:7], None), (pp[1], planes[3:6], (2, 2, 4)), (pc[0], codes[3:7], None),
                             (pp[2], planes[0:2], None), (pc[1], codes[0:3], (4, 2, 2)), (pc[1], planes[2:3], None)):
        need("pool", [tok])
        loc += fused(g, T, topo, "a1", off, jobs, share)
    loc1 = loc
    need("pool", [dt0])
    loc += fused(g, T, topo, "at", on, [(h[0], T.tabd[rank], T.thop[:]) for h in hs])
    t = P(T.m0[:], T.ms[:], [[32, 2], [-K2, 8]], A.is_ge, 0.0, 0, 1)
    IOTA(T.k3[:], [[16, 8], [0, 2], [1, 16]], 0, 0)
    IOTA(T.j3[:], [[32, 2]], 0, 1)
    IOTA(T.b256[:], [[0, 1]], 0, 256)
    need("pool", [t])
    c_k3 = P(T.m1[:], T.m0[:], [[-32, 2], [K2, 8]], A.is_ge, 0.0, K2 - 1, -1)

    wq = V([dw], "qz", T.wq[:], T.ws[:], T.wb[:])
    t = V([c_pi], "ts", T.si[:], T.pi[:], 4, None, A.arith_shift_right)
    t = V([t], "ts", T.bi[:], T.si[:], -1.0, float(rank + N), A.mult, A.add)
    t = V([t], "ts", T.ci[:], T.bi[:], N - 1, None, A.bitwise_and)
    c_key = V([t, c_p8], "ts", T.key[:], T.ci[:], T.p8[:], None, A.add)
    t = V([], "ts", T.pm[:], T.si[:], -16.0, None, A.mult)
    t = V([t, c_k2], "ts", T.jj[:], T.j16[:], T.pm[:], None, A.add)
    t = V([t], "ts", T.jq[:], T.jj[:], 1.0 / K2, 0.5 / K2 - 0.5, A.mult, A.add)
    t = V([t], "ts", T.jr[:], T.jq[:], float(32 - K2), None, A.mult)
    t = V([t], "tt", T.j16[:], T.jr[:], T.jj[:], A.add)
    c_pk = V([t], "copy", T.pk[:], T.j16[:])
    c_tab = [V([], "set", T.tab[:, c128(s)], float(s)) for s in range(N)][-1]

    arr1 = [("a1", loc1), oc, osc]
    L1 = (T.land1[:], T.land1s[:])
    t = MM(arr1 + free1, T.pss[:, 0:128], L1, U)
    tB2 = MM([], T.psb[:, 0:128], U, L1)
    V([tB2], "ts", T.g2[:, 0:128], T.psb[:, 0:128], T.pss[:, 0:1], -1.0, A.is_equal, A.mult)
    e2 = V([], "ts", T.g2[:, 128:256], T.psb[:, 0:128], T.pss[:, 0:1], None, A.is_ge)
    r2 = V([e2], "scan", T.r2[:], T.mk2[:], T.g2[:], 0.0, A.mult, A.add)
    tk = V([r2, c_key], "ts", T.oh2[:, 64:160], T.k2[:, 64:160], T.r2[:, 255:256], T.key[:], A.is_equal, A.mult)
    tp = V([], "ts", T.oh2[:, 0:64], T.k2[:, 0:64], T.r2[:, 255:256], T.pf[:], A.is_equal, A.mult)
    tk = [V([tk], "tr", T.ot2[0:64, 2:5, c128(a, 32)], T.oh2[c128(a, 64), 64:160]) for a in range(2)]
    tp = [V([tp], "tr", T.ot2[0:64, 0:2, c128(a, 32)], T.oh2[c128(a, 64), 0:64]) for a in range(2)]
    tk = sums(tk, T.ot2, T.s2, range(2, 5))
    tp = sums(tp, T.ot2, T.s2, range(2))
    ks = [ACT(tk, T.kl[p:p + 32, rank, 0:3], T.s2[0:32, 2:5, 63], F.Identity, scale=KS) for p in (0, 32, 64, 96)]
    off2 = [V(tp, "copy", T.kb[p:p + 32, :], T.s2[0:32, 0:2, 63]) for p in (0, 32, 64, 96)]
    me2 = c128(rank, K2)
    pc = V(off2 + arr1, "copy", u32(T.snd2[:, 0:32]), u32(T.land1[:]).indirect(T.kb[:, 0:2]))
    psc = ACT(off2 + arr1, T.snd2s[:, 0:32], T.land1s[:].indirect(T.kb[:, 0:2]), F.Copy)
    need("pool", ks)
    far, near = [T.cores[d] for d in hs[0][2]], [T.cores[d] for d in hs[2][2]]
    keys = T.kl[:, rank, 0:3]
    loc += fused(g, T, topo, "ak", off + on, [(d, keys, keys) for d in far[0:2]] + [(hs[2][0], keys, T.hk[:])], (4, 4, 8))
    loc += fused(g, T, topo, "ak", on, [(hs[0][0], keys, T.hk[:])])
    codes, planes = (u8(T.snd2[:, 0:K2]), u8(T.land2[:, me2])), (T.snd2s[:, 0:K2], T.land2s[:, me2])
    need("pool", [psc])
    loc += fused(g, T, topo, "a2", on, [(h[0], planes[0], T.hps[:]) for h in hs[0:2]])
    need("pool", [pc])
    loc += fused(g, T, topo, "a2", on, [(hs[2][0], codes[0], u8(T.hq[:]))])
    loc += fused(g, T, topo, "a2", off, [(d,) + codes for d in far])
    loc += fused(g, T, topo, "a2", off, [(d,) + codes for d in near])
    at = ("at", len(off) * len(hs))
    dt1 = dma("sync", [at, dt0, c_tab], T.tab[1:2, :], T.tabd[:], "dt1")

    ak = ("ak", 4 * len(far) + 2 * (N - 1 - len(far)))
    xr, order = {}, [rank] + [b for b in range(N) if b != rank]
    for i, b in enumerate(order):
        if i < 5:
            xr[b] = V(([ak] if i else [c_k3]) + ks, "ts", T.xr[:, c128(b, 32)], T.z32[:], T.kl[:, b, 0:1], None, A.add)
        else:
            xr[b] = ACT([ak], T.xr[:, c128(b, 32)], T.z32[:], F.Identity, bias=T.kl[:, b, 0:1])
    t = [V([], "tt", T.mk[:, 9 * c:9 * c + 8], T.kl[:, :, 2], T.m1[:, c128(c, 8)], A.mult) for c in range(2)]
    V([xr[b] for b in range(4)], "tr", T.idr[:, 0:4, :], T.xr[:, 0:128])
    idr = V([xr[b] for b in range(4, 8)], "tr", T.idr[:, 4:8, :], T.xr[:, 128:256])
    kp = [V([t[c]], "red", T.kp[:, c:c + 1], T.mk[:, c128(c, 9)], AxisListType.X, A.add) for c in range(2)]
    koff = V([], "ts", T.koff[:], T.kl[:, :, 0:2], 1.0 / KS, None, A.mult)
    num = ACT([koff, dt1], T.num[:], T.tab[:].indirect(T.koff[:]), F.Copy)
    lanes = (slice(0, 128), slice(96, 128))

    arr2 = [("a2", 5 * len(off))]
    L2 = (T.land2[:], T.land2s[:])
    tS3 = [MM(arr2 + [e2] + free1, T.pss[:, 512:640], (T.land2[:, 0:128], T.land2s[:, 0:128]), U)]
    tB3 = MM([], T.psb[:, 512:512 + M], U, L2)
    tS3.append(MM([], T.pss[:, 1024:1152], (T.land2[:, 32:M], T.land2s[:, 32:M]), U))
    yps = [T.psb[:, 1024:1024 + M], T.psb[:, 1536:1536 + M], T.pss[:, 1536:1536 + M]]
    tY = [MM([wq], yps[o], (T.wq[:, c128(o)], T.ws[:, c128(o)]), L2) for o in range(3)]
    nump = ACT([num, c_pk], T.nump[:], T.num[:].indirect(T.pk[:]), F.Copy)
    ysb = [ACT([tY[o]], T.ysb[:, c128(o, M)], yps[o], F.Copy) for o in range(3)]
    st3, g3, e3, r3, oh3 = {}, {}, {}, {}, {}
    own = [T.pss[lanes[c], 512 * c + 512:512 * c + 513] for c in range(2)]

    def first(c):
        st3[c] = V([tS3[c], idr] + kp, "ts", T.st3[lanes[c], c128(c, M)], T.idr[lanes[c], :, 0:K2], T.kp[lanes[c], c:c + 1], own[c], A.add, A.max)

    def larger(c):
        g3[c] = V([tB3, tS3[c]], "ts", T.g3[lanes[c], c128(2 * c, M)], T.psb[lanes[c], 512:512 + M], own[c], None, A.is_gt)

    def equal(c):
        e3[c] = V([st3[c]], "tt", T.g3[lanes[c], c128(2 * c + 1, M)], T.psb[lanes[c], 512:512 + M], T.st3[lanes[c], c128(c, M)], A.is_equal)

    for step, c in ((first, 0), (larger, 0), (first, 1), (equal, 0), (larger, 1), (equal, 1)):
        step(c)
    for c in range(2):
        r3[c] = V([g3[c], e3[c]], "scan", T.r3[lanes[c], c128(c, M)], T.g3[lanes[c], c128(2 * c, M)], T.g3[lanes[c], c128(2 * c + 1, M)], 0.0, A.add, A.add)
    for c, a, n in ((0, 0, 256), (1, 0, 128), (1, 128, 128)):
        oh3[c, a] = V([r3[c]], "ts", T.oh3[lanes[c], 256 * c + a:256 * c + a + n], T.k3[lanes[c], a:a + n], T.r3[lanes[c], M * c + M - 1:M * c + M],
                      T.j3[lanes[c], c:c + 1], A.is_equal, A.mult)
    V([oh3[0, 0]], "tr", T.ot3[0:64, 0:4, 0:32], T.oh3[0:64, 0:128])
    V([], "tr", T.ot3[0:64, 0:4, 32:64], T.oh3[64:128, 0:128])
    V([], "tr", T.ot3[0:64, 4:8, 0:32], T.oh3[0:64, 128:256])
    ta = V([oh3[1, 0]], "tr", T.ot3[0:32, 0:4, 64:96], T.oh3[96:128, 256:384])
    V([], "tr", T.ot3[0:64, 4:8, 32:64], T.oh3[64:128, 128:256])
    tb = V([oh3[1, 128]], "tr", T.ot3[0:32, 4:8, 64:96], T.oh3[96:128, 384:512])
    t = sums([ta], T.ot3, T.sm3, range(4)) + sums([tb], T.ot3, T.sm3, range(4, 8))
    off3 = [V(t, "copy", T.off3[p:p + 32, :], T.sm3[0:32, :, 95]) for p in (0, 32, 64, 96)]
    y0 = V(off3 + ysb, "copy", T.yo[:, c128(0)], T.ysb[:, c128(0, M)].indirect(T.off3[:]))
    y1 = ACT(off3 + ysb, T.yo[:, c128(1)], T.ysb[:, c128(1, M)].indirect(T.off3[:]), F.Copy)
    y2 = V([], "copy", T.yo[:, c128(2)], T.ysb[:, c128(2, M)].indirect(T.off3[:]))
    ido = ACT([nump, c_k3], T.ido[:], T.nump[:].indirect(T.off3[:]), F.Identity, bias=T.b256[:])
    outs = [dma("sync", [y0, y1], T.y[:, 0:256], T.yo[:, 0:256], "dy0"), dma("sync", [y2], T.y[:, c128(2)], T.yo[:, c128(2)], "dy1"),
            dma("sca", [ido], T["id"][:], T.ido[0:2, :], "di")]
    need("pool", list(cnt.items()) + arr1 + arr2 + [ak, at, dt1, ("loc", loc), du, dw] + dx + outs)
